import numpy as np
CORES = [2,3,6,7,58,59,62,63,114,115,118,119]
N = 12
R, E = 8192, 2048
CAPP = 512
def entries(a): return a.T.reshape(-1)
def pack(v, P): return np.ascontiguousarray(np.asarray(v, np.int32).reshape(-1, P).T)
def lists(rng, how):
    n = N * E; q = np.arange(n) // E
    P = rng.permutation(np.repeat(np.arange(N * N), CAPP))[:n]
    if how == "full":
        a = rng.integers(0, N); z = np.delete(np.arange(N), a); o = rng.permutation(N * N); o = o[(o // N != a) & (o % N != a) & (o // N != o % N)]
        C = np.concatenate([N * a + rng.permutation(z), [(N + 1) * a], N * rng.permutation(z) + a, o])[:n // CAPP]
        L = np.repeat(C, CAPP).reshape(N, E); s, t = 1 + 2 * rng.integers(0, CAPP // 8, 2); t += 2 * (CAPP // 8)
        L[0, :s], L[1, :s] = C[E // CAPP], C[0]; L[0, s:s + t], L[N - 1, E - t:] = C[-1], C[0]
        L = L[rng.permutation(N)]; L[0] = L[0].reshape(16, -1).T.reshape(-1)
        for r in range(1, N, 2): L[r] = rng.permutation(L[r])
        P = L.reshape(-1)
    if how == "same":
        o = np.arange(N * N); o = rng.permutation(np.repeat(o[o % (N + 1) != 0], CAPP))[:n - N * CAPP].reshape(N, E - CAPP)
        P = np.stack([rng.permutation(np.append(o[r], np.full(CAPP, (N + 1) * r))) for r in range(N)]).reshape(-1)
    if how == "cross":
        d = np.stack([rng.permutation(1 + np.arange(E) % (N - 1)) for r in range(N)]).reshape(-1); a = 1 + rng.integers(0, N - 2, N); a += a >= N - np.arange(N)
        P = (q + a[d]) % N * N + (q + a[d] + d) % N
    if how == "edge": k = rng.permutation(n); P = k % (N * N)
    h, g = P // N, P % N; u, v = rng.integers(0, R, n), rng.integers(0, R, n)
    if how == "alike": u, v = rng.integers(0, R, N * N)[P], rng.integers(0, R, N * N)[P]
    if how == "edge": u, v = (R - 1) * (k // (N * N) % 2), (R - 1) * (k // (2 * N * N) % 2)
    if how == "full": u, v = (np.stack([rng.permutation(R)[np.arange(E) % R] for r in range(N)]).reshape(-1) for _ in range(2))
    if how == "same": v = u
    return {"pi": np.stack([pack(w, 16) for w in (R * h + u).reshape(N, E)]), "pj": np.stack([pack(w, 16) for w in (R * g + v).reshape(N, E)])}
def setup_inputs(rng):
    return dict({"ta": rng.standard_normal((N, 128, R), dtype=np.float32), "tb": rng.standard_normal((N, 128, R), dtype=np.float32)}, **lists(rng, "uniform"))
def setup_inputs_alike(rng):
    d = setup_inputs(rng); d.update(lists(rng, "alike"))
    for k in ("ta", "tb"): d[k] = (d[k].astype(np.float32) * 1024.0).astype(d[k].dtype)
    return d
def setup_inputs_cross(rng):
    d = setup_inputs(rng); d.update(lists(rng, "cross"))
    for k in ("ta", "tb"): d[k] = (d[k].astype(np.float32) * (1 / 1024.0)).astype(d[k].dtype)
    return d
def setup_inputs_edge(rng):
    d = setup_inputs(rng); d.update(lists(rng, "edge"))
    return d
def setup_inputs_full(rng):
    d = setup_inputs(rng); d.update(lists(rng, "full"))
    return d
def setup_inputs_same(rng):
    d = setup_inputs(rng); d.update(lists(rng, "same"))
    return d
def check_inputs(x):
    bad = []
    if x["pi"].min() < 0 or x["pi"].max() >= N * R: bad.append("pi out of range")
    if x["pj"].min() < 0 or x["pj"].max() >= N * R: bad.append("pj out of range")
    if not bad and int(np.bincount((x["pi"] // R * N + x["pj"] // R).reshape(-1), minlength=N * N).max()) > CAPP: bad.append("more than CAPP pairs with i in one rank's part of TA and j in one rank's part of TB")
    return bad
def reference(ta, tb, pi, pj):
    A, B = np.concatenate(list(ta), axis=1).astype(np.float64), np.concatenate(list(tb), axis=1).astype(np.float64)
    y = []
    for r in range(N):
        i, j = entries(pi[r]), entries(pj[r])
        y.append((A[:, i] * B[:, j]).sum(axis=0))
    return {"y": np.stack(y).reshape(N, -1, 16).transpose(0, 2, 1).astype(np.float32)}

@@ -1,0 +1,468 @@
+from concourse.bass import DstId, RemoteDMATransfer
+from concourse.mybir import AluOpType as OP, ActivationFunctionType as AF
+
+NR, RC, CAP, H6, NC = 12, 8192, 512, 6, 96
+SLOTS = NR * CAP
+DUMP = 16 * NC
+WIN = SLOTS + DUMP
+
+SCRATCH = {
+    "rawi": ("dram", [128, 16], "int32"), "rawj": ("dram", [128, 16], "int32"),
+    "rini": ("dram", [H6, 128, 16], "int32"), "rinj": ("dram", [H6, 128, 16], "int32"),
+    "dres": ("dram", [NR, 128, 16], "float32"),
+    "sta": ("sbuf", [128, RC], "float32"), "stb": ("sbuf", [128, RC], "float32"),
+    "sb": ("sbuf", [128, SLOTS], "float32"), "rb": ("sbuf", [128, SLOTS], "float32"),
+    "wa": ("sbuf", [128, WIN], "bfloat16"), "wb": ("sbuf", [128, WIN], "bfloat16"),
+    "sw": ("sbuf", [128, WIN], "float32"),
+    "r0": ("sbuf", [128, DUMP], "float32"), "r1": ("sbuf", [128, DUMP], "float32"),
+    "va": ("sbuf", [128, DUMP], "bfloat16"), "vb": ("sbuf", [128, DUMP], "bfloat16"),
+    "oh": ("sbuf", [128, NR * NC], "bfloat16"), "onesb": ("sbuf", [128, NR * NC], "bfloat16"),
+    "ms": ("sbuf", [128, 576], "float32"), "t1": ("sbuf", [128, 576], "float32"), "t2": ("sbuf", [128, 288], "float32"),
+    "prod": ("sbuf", [128, 2 * CAP], "float32"),
+    "lb": ("sbuf", [128, 16 * 128], "bfloat16"), "zz": ("sbuf", [128, 16 * 132], "bfloat16"),
+    "li": ("sbuf", [128, NC], "int32"), "lj": ("sbuf", [128, NC], "int32"),
+    "i96": ("sbuf", [128, 6 * NC], "int32"), "b96": ("sbuf", [128, 6 * NC], "bfloat16"), "f96": ("sbuf", [128, 8 * NC], "float32"),
+    "ee": ("sbuf", [128, 16], "float32"), "e0": ("sbuf", [128, 12], "float32"), "tt": ("sbuf", [128, 12], "bfloat16"),
+    "base": ("sbuf", [128, 12], "float32"), "cb": ("sbuf", [128, 12], "float32"),
+    "sla": ("sbuf", [128, NC], "uint16"), "slb": ("sbuf", [128, NC], "uint16"), "slp": ("sbuf", [128, NC], "uint16"),
+    "xa": ("sbuf", [128, NC], "bfloat16"), "xb": ("sbuf", [128, NC], "bfloat16"),
+    "xpa": ("sbuf", [128, NC], "bfloat16"), "xpb": ("sbuf", [128, NC], "bfloat16"),
+    "offa": ("sbuf", [128, 384], "uint16"), "offb": ("sbuf", [128, 384], "uint16"),
+    "i16": ("sbuf", [128, 48], "int32"), "f16": ("sbuf", [128, 64], "float32"), "sel": ("sbuf", [128, 16], "bfloat16"),
+    "mask8": ("sbuf", [128, 8], "float32"),
+    "i128": ("sbuf", [128, 256], "int32"), "mmf": ("sbuf", [128, 128], "float32"),
+    "rep16": ("sbuf", [128, 128], "bfloat16"), "dd": ("sbuf", [128, 148], "float32"), "idz": ("sbuf", [128, 148], "bfloat16"),
+    "tri": ("sbuf", [128, 128], "bfloat16"), "ident": ("sbuf", [128, 128], "float32"), "onesf": ("sbuf", [128, 128], "float32"),
+    "res": ("sbuf", [128, NR * 16], "float32"), "ss": ("sbuf", [128, 192], "float32"), "ys": ("sbuf", [16, 128], "float32"),
+    "cum": ("psum", [128, 1536], "float32"), "sc0": ("psum", [128, 512], "float32"), "sc1": ("psum", [128, 512], "float32"),
+    "un": ("psum", [128, 512], "float32"), "sm": ("psum", [128, 512], "float32"), "ofp": ("psum", [128, 512], "float32"),
+}
+SEMAPHORES = (["v", "a", "p", "gp", "draw", "dself", "dl", "dl2", "dta0", "dta1", "dtb", "dd0", "dd1", "dd2", "dy",
+               "rawin", "rawsent", "xpa", "xpb", "slp", "xsent", "psent", "ressent", "resin", "rlsent"]
+              + ["pay%d" % k for k in range(NR)] + ["rl%d" % k for k in range(4)])
+
+
+def bits(mask):
+    return [1 << b for b in range(mask.bit_length()) if mask >> b & 1]
+
+
+def plan(cores, topo):
+    n = len(cores)
+    chips = sorted({topo.chip(c) for c in cores})
+    ncore = 8 * 16
+    partner = {}
+    taken = set(cores)
+    for c in cores:
+        p = [d for d in range(ncore) if topo.chip(d) == topo.chip(c) and topo.die(d) == topo.die(c) and d not in taken][0]
+        taken.add(p)
+        partner[c] = p
+    x, y = [(a, b) for a in chips for b in chips if a < b and topo.same_plane(a, b)][0]
+    z = [c for c in chips if c not in (x, y)][0]
+    relayed = {(y, x), (y, z), (z, y)}
+    relay = {}
+    for s in cores:
+        for d in cores:
+            if (topo.chip(s), topo.chip(d)) not in relayed:
+                continue
+            peers = [c for c in cores if topo.chip(c) == topo.chip(s) and topo.die(c) == topo.die(s)]
+            cand = [r for r in range(ncore) if topo.mates(topo.chip(r), topo.chip(d)) and topo.die(r) == topo.die(s)
+                    and all(topo.may_write(r, e) for e in cores if topo.chip(e) == topo.chip(d))]
+            relay[s, d] = cand[peers.index(s) % len(cand)]
+    order = []
+    for h in range(n):
+        s = cores[h]
+        far = [[b for b in range(n) if topo.chip(cores[b]) == ch] for ch in chips if ch != topo.chip(s)]
+        far.sort(key=lambda L: (s, cores[L[0]]) not in relay)
+        near = [b for b in range(n) if b != h and topo.chip(cores[b]) == topo.chip(s)]
+        far = [L[h % 4:] + L[:h % 4] for L in far]
+        near = near[h % 3:] + near[:h % 3]
+        o = []
+        for k in range(4):
+            o += [far[0][k], far[1][k]] + near[k:k + 1]
+        order.append(o + [h])
+    return partner, relay, order
+
+
+def rank_program(g, core, T, topo):
+    cores = list(T.cores)
+    partner, relay, order = plan(cores, topo)
+    owner_of = {p: c for c, p in partner.items()}
+    S = T.sem
+    V, A, P, Y = g.vector, g.scalar, g.tensor, g.sync
+    rank = T.rank_of(core)
+
+    def dst(c):
+        rid, pid, _ = topo.addr(c)
+        return rid, pid
+
+    if rank is None and core not in owner_of:
+        jobs = [(s, d) for (s, d), r in relay.items() if r == core]
+        if not jobs:
+            return
+        s = jobs[0][0]
+        h = cores.index(s)
+        jobs.sort(key=lambda sd: order[h].index(cores.index(sd[1])))
+        for _, d in jobs:
+            k = slot_at_relay(cores, topo, d)
+            g.wait_ge(S["rl%d" % k], 8)
+            rid, pid = dst(d)
+            g.remote_dma(out_ap=T.rb[:, CAP * h:CAP * h + CAP], in_ap=T.rb[:, CAP * k:CAP * k + CAP],
+                         remote_sem=S["pay%d" % h], local_sem=S["rlsent"], pid=pid, routing_id=rid,
+                         dma_engine_mask=topo.mask(core, d))
+        g.wait_ge(S["rlsent"], 8 * len(jobs))
+        return
+
+    own = core if rank is not None else owner_of[core]
+    me = cores.index(own)
+    half = 0 if rank is not None else 1
+    is_owner = half == 0
+    cnt = {}
+    seen = {}
+
+    def cut(buf, n, names):
+        return {name: buf[:, n * k:n * k + n] for k, name in enumerate(names)}
+
+    B = {}
+    B.update(cut(T.i96, NC, ["hi", "hj", "xi", "xj", "xh", "xk"]))
+    B.update(cut(T.b96, NC, ["lo_a", "hi_a", "lo_b", "hi_b", "key", "keyb"]))
+    B.update(cut(T.f96, NC, ["tk", "nm", "dmp", "dump0", "dumpc", "t3", "t4", "t5"]))
+    B.update(cut(T.i16, 16, ["ip", "pm", "pg"]))
+    B.update(cut(T.f16, 16, ["pmf", "pgf", "ir", "mask16"]))
+    B.update(cut(T.i128, 128, ["im", "mm"]))
+    pcol = T.f16[:, 0:1]
+
+    def wait(q, qn, deps):
+        for t in deps:
+            if t is None:
+                continue
+            name, n = t
+            if seen.get((qn, name), 0) >= n:
+                continue
+            seen[qn, name] = n
+            q.wait_ge(S[name], n)
+
+    def mk(qn):
+        def tok(inst):
+            cnt[qn] = cnt.get(qn, 0) + 1
+            inst.then_inc(S[qn], 1)
+            return (qn, cnt[qn])
+        return tok
+
+    vt, at, pt, gt = mk("v"), mk("a"), mk("p"), mk("gp")
+
+    def dma(q, qn, out, in_, sem, deps=()):
+        wait(q, qn, deps)
+        q.dma_start(out, in_).then_inc(S[sem], 16)
+        cnt[sem] = cnt.get(sem, 0) + 16
+        return (sem, cnt[sem])
+
+    def ts(out, in0, s1, s2, op0, op1=None, deps=()):
+        wait(V, "v", deps)
+        if op1 is None:
+            return vt(V.tensor_scalar(out, in0, s1, None, op0))
+        return vt(V.tensor_scalar(out, in0, s1, s2, op0, op1))
+
+    def tt(out, in0, in1, op, deps=()):
+        wait(V, "v", deps)
+        return vt(V.tensor_tensor(out, in0, in1, op))
+
+    def vcopy(out, in_, deps=()):
+        wait(V, "v", deps)
+        return vt(V.tensor_copy(out, in_))
+
+    def ms(ap, c, deps=()):
+        wait(V, "v", deps)
+        return vt(V.memset(ap, c))
+
+    def mm(out, lhsT, rhs, start=True, stop=True, deps=()):
+        wait(P, "p", deps)
+        return pt(P.matmul(out, lhsT, rhs, start, stop))
+
+    def act(out, in_, deps=()):
+        wait(A, "a", deps)
+        return at(A.activation(out, in_, AF.Copy))
+
+    tself = None
+    nraw = 8 * H6
+    if is_owner:
+        ql, to = rank % H6, (cores if rank < H6 else [partner[c] for c in cores])
+        dma(Y, "y", T.rawi[:], T.pi[:], "draw")
+        dma(A, "a", T.rawj[:], T.pj[:], "draw")
+        if rank < H6:
+            dma(Y, "y", T.rini[ql], T.pi[:], "dself")
+            tself = dma(A, "a", T.rinj[ql], T.pj[:], "dself")
+            nraw -= 8
+        wait(g, "g", [("draw", 32)])
+        off = [c for c in to if topo.chip(c) != topo.chip(core)]
+        on = [c for c in to if topo.chip(c) == topo.chip(core) and c != core]
+        mo = topo.mask(core, off[0])
+        mn = topo.mask(core, on[0]) & ~mo
+        tr = []
+        for dl, mk_ in ((off, mo), (on, mn)):
+            b = bits(mk_)
+            ids = []
+            for c in dl:
+                rid, pid = dst(c)
+                ids.append(DstId(rid=rid, pnc=pid))
+            for src, buf, eng in ((T.rawi, T.rini, b[:4]), (T.rawj, T.rinj, b[4:8])):
+                tr.append(RemoteDMATransfer(dst_ids=ids, dma_engine_mask=sum(eng), remote_sem=S["rawin"],
+                                            srcs=[src[:]], dsts=[buf[ql] for _ in ids], alu_op=0))
+        g.remote_dma_fused(tr, local_sem=S["rawsent"])
+        dma(Y, "y", T.sta[:, 0:1024], T.ta[:, 0:1024], "dta0", deps=[("rawsent", 16)])
+
+    F = {"allow_small_or_imprecise_dtypes": True}
+    c_ip = gt(g.iota(B["ip"], [[0, 16]], 0, 1))
+    c_ir = gt(g.iota(B["ir"], [[1, 16]], 0, 0, **F))
+    c_dd = gt(g.iota(T.dd[:], [[1, 148]], -1, -1, **F))
+    c_du = gt(g.iota(B["dump0"], [[16, NC]], SLOTS, 0, **F))
+    c_cb = gt(g.iota(T.cb[:], [[CAP, 12]], -1 if is_owner else CAP, 0, **F))
+    if is_owner:
+        c_im = gt(g.iota(B["im"], [[1, 128]], 0, 0))
+    zwa = ms(T.wa[:, 0:SLOTS], 0.0)
+    k_ob = ms(T.onesb[:], 1.0)
+    k_ee = ms(T.ee[:], 0.0)
+    k_pm = ts(B["pm"], B["ip"], 15, None, OP.bitwise_and, deps=[c_ip])
+    k_pmf = vcopy(B["pmf"], B["pm"], deps=[k_pm])
+    k_id = ts(T.idz[:], T.dd[:], 0.0, None, OP.is_equal, deps=[c_dd])
+    k_tri = ts(T.tri[:], T.dd[:, 1:129], 0.0, None, OP.is_gt)
+    k_m16 = tt(B["mask16"], B["pmf"], B["ir"], OP.is_equal, deps=[k_pmf, c_ir])
+    k_sel = tt(T.sel[:], B["pmf"], B["ir"], OP.is_equal)
+    k_du = ts(B["dumpc"], B["dump0"], pcol, None, OP.add, deps=[c_du])
+    for r in range(16):
+        k_z = ts(T.zz[:, 132 * r:132 * r + 130], T.idz[:, r:r + 130], T.f16[:, 48 + r:49 + r], None, OP.mult,
+                 deps=[k_m16, k_id])
+    if is_owner:
+        k_pg = ts(B["pg"], B["ip"], 4, None, OP.arith_shift_right)
+        k_mm = ts(B["mm"], B["im"], 15, None, OP.bitwise_and, deps=[c_im])
+        k_pgf = vcopy(B["pgf"], B["pg"], deps=[k_pg])
+        k_mmf = vcopy(T.mmf[:], B["mm"], deps=[k_mm])
+        k_m8 = tt(T.mask8[:], T.f16[:, 16:24], T.f16[:, 32:40], OP.is_equal, deps=[k_pgf])
+        k_rep = ts(T.rep16[:], T.mmf[:], pcol, None, OP.is_equal, deps=[k_mmf])
+        for b in range(8):
+            for w in range(2):
+                k_lb = ts(T.lb[:, 128 * (2 * b + w):128 * (2 * b + w) + 128], T.rep16[:], T.mask8[:, b:b + 1],
+                          1.0 if w else 64.0, OP.mult, OP.mult, deps=[k_rep, k_m8])
+        k_of = ms(T.onesf[:], 1.0)
+        k_idf = ts(T.ident[:], T.dd[:, 1:129], 0.0, None, OP.is_equal)
+
+    for q, qn, src, out, sem in ((Y, "y", T.rini, T.li, "dl"), (A, "a", T.rinj, T.lj, "dl2")):
+        wait(q, qn, [("rawin", nraw), ("dself", 32) if tself else None])
+        dma(q, qn, out[0:96, :], src[:, 0:96, :], sem)
+        for k in range(H6):
+            p0 = 96 + 16 * (k // 3)
+            dma(q, qn, out[p0:p0 + 16, 32 * (k % 3):32 * (k % 3) + 32], src[k, 96:128, :], sem)
+    l_i, l_j = ("dl", cnt["dl"]), ("dl2", cnt["dl2"])
+    if is_owner:
+        for a in range(1, 8):
+            t_ta = dma(Y, "y", T.sta[:, 1024 * a:1024 * a + 1024], T.ta[:, 1024 * a:1024 * a + 1024], "dta1")
+        for a in range(4):
+            t_tb = dma(Y, "y", T.stb[:, 2048 * a:2048 * a + 2048], T.tb[:, 2048 * a:2048 * a + 2048], "dtb")
+
+    ts(B["xi"], T.li[:], 63, None, OP.bitwise_and, deps=[l_i])
+    ts(B["xh"], T.li[:], 6, 127, OP.logical_shift_right, OP.bitwise_and)
+    b_hi = ts(B["hi"], T.li[:], 13, None, OP.logical_shift_right)
+    vcopy(B["lo_a"], B["xi"], deps=[b_hi])
+    b_ha = vcopy(B["hi_a"], B["xh"])
+    ts(B["hj"], T.lj[:], 13, None, OP.logical_shift_right, deps=[l_j])
+    b_t = ts(B["tk"], B["hi"], float(me), 16.0, OP.not_equal, OP.mult)
+    k_key = tt(B["key"], B["tk"], B["hj"], OP.add, deps=[b_t])
+
+    banks = [T.sc0, T.sc1, T.un]
+    bank_free = [None, None, None]
+
+    def unwrap(lo, hi, out, blocks, dep):
+        last = None
+        for blk in blocks:
+            bk = banks[blk % 3]
+            for k in range(4):
+                r = 4 * blk + k
+                o = bk[:, NC * k:NC * k + NC]
+                mm(o, T.zz[:, 132 * r + 1:132 * r + 129], hi, True, False, deps=[dep, k_z, bank_free[blk % 3]])
+                last = mm(o, T.zz[:, 132 * r:132 * r + 128], lo, False, True)
+            for k in range(4):
+                r = 4 * blk + k
+                bank_free[blk % 3] = act(out[:, r:DUMP:16], bk[:, NC * k:NC * k + NC], deps=[last])
+        return bank_free[blocks[-1] % 3]
+
+    def rank1(key, dep, pdep):
+        nm = ts(B["nm"], key, 16.0, None, OP.is_ge, deps=[dep])
+        for c in range(NR):
+            o = ts(T.oh[:, NC * c:NC * c + NC], key, float(c), None, OP.is_equal, deps=[pdep])
+        dm = tt(B["dmp"], B["nm"], B["dumpc"], OP.mult, deps=[nm, k_du])
+        return o, dm
+
+    def rank2(o, dm, pdep):
+        wait(V, "v", [o, k_ob, k_ee])
+        s = vt(V.tensor_tensor_scan(T.cum[:, 0:NR * NC], T.onesb[:], T.oh[:], 0.0, OP.mult,
+                                    OP.add if is_owner else OP.subtract))
+        e = vcopy(T.ee[:, 1:13], T.cum[:, NC - 1:NR * NC:NC], deps=[s])
+        t = tt(T.tt[:], T.ee[:, 1:13], T.ee[:, 0:12], OP.subtract, deps=[e])
+        e0 = tt(T.e0[:], T.ee[:, 0:12], T.cb[:], OP.subtract, deps=[c_cb])
+        m = mm(T.sm[:, 0:12], T.tri[:], T.tt[:], deps=[t, k_tri, pdep])
+        return e0, m
+
+    def rank3(e0, m, dm, sl):
+        b = tt(T.base[:], T.sm[:, 0:12], T.e0[:], OP.subtract, deps=[m, e0])
+        for c in range(NR):
+            o = ts(T.cum[:, NC * c:NC * c + NC], T.cum[:, NC * c:NC * c + NC], T.base[:, c:c + 1], None, OP.add, deps=[b])
+        tt(T.ms[:], T.cum[:, 576:1152], T.oh[:, 576:1152], OP.mult, deps=[o])
+        m1 = tt(T.cum[:, 0:576], T.cum[:, 0:576], T.oh[:, 0:576], OP.mult)
+        a1 = tt(T.t1[:], T.cum[:, 0:576], T.ms[:], OP.add, deps=[m1])
+        a2 = tt(T.t2[:], T.t1[:, 0:288], T.t1[:, 288:576], OP.add, deps=[a1])
+        tt(B["t3"], T.t2[:, 0:96], T.t2[:, 96:192], OP.add, deps=[a2])
+        a4 = tt(B["t4"], T.t2[:, 192:288], B["dmp"], OP.add, deps=[dm])
+        a5 = tt(B["t5"], B["t3"], B["t4"], OP.add, deps=[a4])
+        return vcopy(sl[:], B["t5"], deps=[a5])
+
+    def scatter(win, sl, vals, deps):
+        wait(V, "v", deps)
+        return vt(V.tensor_copy(win[:, 0:WIN].indirect(sl[:, 0:NC]), vals[:]))
+
+    def wrap1(win, dep, free):
+        for ch in range(48):
+            t = mm(T.sm[:, 32 + 2 * ch:34 + 2 * ch], win[:, 128 * ch:128 * ch + 128], T.sel[:, 0:2], deps=[dep, k_sel, free])
+        return t
+
+    def wrap2(x, dep, free):
+        for b in range(8):
+            o = T.ofp[:, b:384:8]
+            mm(o, T.lb[:, 256 * b:256 * b + 128], x[:, 0:NC:2], True, False, deps=[dep, k_lb, free])
+            t = mm(o, T.lb[:, 256 * b + 128:256 * b + 256], x[:, 1:NC:2], False, True)
+        return t
+
+    unwrap(B["lo_a"], B["hi_a"], T.va, [0, 1, 2], b_ha)
+    o, dm = rank1(B["key"], k_key, None)
+    e0, m = rank2(o, dm, None)
+    u_a = unwrap(B["lo_a"], B["hi_a"], T.va, [3], b_ha)
+    ts(B["xj"], T.lj[:], 63, None, OP.bitwise_and)
+    b_hk = ts(B["xk"], T.lj[:], 6, 127, OP.logical_shift_right, OP.bitwise_and)
+    vcopy(B["lo_b"], B["xj"], deps=[b_hk])
+    b_hb = vcopy(B["hi_b"], B["xk"])
+    sl_a = rank3(e0, m, dm, T.sla)
+    u_b = unwrap(B["lo_b"], B["hi_b"], T.vb, [0, 1, 2, 3], b_hb)
+    sc_a = scatter(T.wa, T.sla, T.va, [sl_a, u_a, zwa])
+    w_a = wrap1(T.wa, sc_a, None)
+    zwb = ms(T.wb[:, 0:SLOTS], 0.0)
+    b_t = ts(B["tk"], B["hj"], float(me), 16.0, OP.not_equal, OP.mult)
+    k_kb = tt(B["keyb"], B["tk"], B["hi"], OP.add, deps=[b_t])
+
+    if not is_owner:
+        x_a = vcopy(T.xa[:], T.sm[:, 32:128], deps=[w_a])
+        rid, pid = dst(own)
+
+        def send(buf, src, name, dep):
+            wait(g, "g", [dep])
+            g.remote_dma(out_ap=buf[:], in_ap=src[:], remote_sem=S[name], local_sem=S["xsent"], pid=pid,
+                         routing_id=rid, dma_engine_mask=topo.mask(core, own))
+
+        send(T.xpa, T.xa, "xpa", x_a)
+        o, dm = rank1(B["keyb"], k_kb, None)
+        e0, m = rank2(o, dm, x_a)
+        sl_b = rank3(e0, m, dm, T.slb)
+        sc_b = scatter(T.wb, T.slb, T.vb, [sl_b, u_b, zwb])
+        w_b = wrap1(T.wb, sc_b, None)
+        x_b = vcopy(T.xb[:], T.sm[:, 32:128], deps=[w_b])
+        send(T.xpb, T.xb, "xpb", x_b)
+        send(T.slp, T.slb, "slp", sl_b)
+        wait(g, "g", [(k, cnt[k]) for k in ("v", "a", "p", "gp")])
+        wait(g, "g", [("xsent", 48)])
+        return
+
+    o, dm = rank1(B["keyb"], k_kb, None)
+    x_a = tt(T.xa[:], T.sm[:, 32:128], T.xpa[:], OP.add, deps=[w_a, ("xpa", 16)])
+    p_a = wrap2(T.xa, x_a, None)
+    e0, m = rank2(o, dm, x_a)
+    o_a = vcopy(T.offa[:], T.ofp[:, 0:384], deps=[p_a])
+
+    full = {}
+    nsentp = 0
+    for b in order[me]:
+        tg = act(T.sb[:, CAP * b:CAP * b + CAP], T.sta[:, 0:RC].indirect(T.offa[:, 32 * b:32 * b + 32]),
+                 deps=[o_a, ("dta0", 16), t_ta])
+        full[b] = tg
+        if b == me:
+            continue
+        d = cores[b]
+        wait(g, "g", [tg])
+        if (core, d) in relay:
+            to = relay[core, d]
+            k = slot_at_relay(cores, topo, d)
+            out, sem = T.rb[:, CAP * k:CAP * k + CAP], "rl%d" % k
+        else:
+            to = d
+            out, sem = T.rb[:, CAP * me:CAP * me + CAP], "pay%d" % me
+        mask = topo.mask(core, to)
+        if topo.chip(to) == topo.chip(core):
+            mask &= ~mo
+        rid, pid = dst(to)
+        g.remote_dma(out_ap=out, in_ap=T.sb[:, CAP * b:CAP * b + CAP], remote_sem=S[sem], local_sem=S["psent"],
+                     pid=pid, routing_id=rid, dma_engine_mask=mask)
+        nsentp += 8
+
+    sl_b = rank3(e0, m, dm, T.slb)
+    sc_b = scatter(T.wb, T.slb, T.vb, [sl_b, u_b, zwb])
+    w_b = wrap1(T.wb, sc_b, None)
+    zsw = ms(T.sw[:, SLOTS:WIN], 0.0)
+    x_b = tt(T.xb[:], T.sm[:, 32:128], T.xpb[:], OP.add, deps=[w_b, ("xpb", 16)])
+    p_b = wrap2(T.xb, x_b, o_a)
+    o_b = vcopy(T.offb[:], T.ofp[:, 0:384], deps=[p_b])
+
+    def arrival(h):
+        if h == me:
+            return 0
+        return order[h].index(me) + (3 if (cores[h], core) in relay else 0)
+
+    scs = [T.sc0, T.sc1]
+    pm_, pc_ = [None, None], [u_b, u_b]
+    for n, h in enumerate(sorted(range(NR), key=lambda h: (arrival(h), h))):
+        k = n % 2
+        pr = T.prod[:, CAP * k:CAP * k + CAP]
+        blk = T.rb
+        if h == me:
+            blk = T.sb
+        wait(V, "v", [o_b, t_tb, full[me] if h == me else ("pay%d" % h, 8), pm_[k]])
+        t = vt(V.tensor_tensor(pr, T.stb[:, 0:RC].indirect(T.offb[:, 32 * h:32 * h + 32]),
+                               blk[:, CAP * h:CAP * h + CAP], OP.mult))
+        pm_[k] = mm(scs[k][:], T.onesf[:], pr, deps=[t, k_of, pc_[k]])
+        pc_[k] = act(T.sw[:, CAP * h:CAP * h + CAP], scs[k][:], deps=[pm_[k]])
+
+    wait(V, "v", [pc_[0], pc_[1], zsw, sl_b])
+    f0 = vt(V.tensor_copy(T.r0[:], T.sw[:, 0:WIN].indirect(T.slb[:, 0:NC])))
+    wait(A, "a", [pc_[0], pc_[1], zsw, ("slp", 16)])
+    f1 = at(A.activation(T.r1[:], T.sw[:, 0:WIN].indirect(T.slp[:, 0:NC]), AF.Copy))
+    for q, qn, R, f, sem, d0 in ((Y, "y", T.r0, f0, "dd0", 0), (A, "a", T.r1, f1, "dd1", H6)):
+        wait(q, qn, [f])
+        dma(q, qn, T.dres[d0:d0 + 6, 0:96, :], R[0:96:16, :], sem)
+        dma(q, qn, T.dres[d0:d0 + 3, 96:128, :], R[96:97, :], sem)
+        dma(q, qn, T.dres[d0 + 3:d0 + 6, 96:128, :], R[112:113, :], sem)
+    td = [("dd0", 48), ("dd1", 48)]
+    wait(g, "g", td)
+    offr = [b for b in range(NR) if topo.chip(cores[b]) != topo.chip(core)]
+    onr = [b for b in range(NR) if topo.chip(cores[b]) == topo.chip(core) and b != me]
+    nres, mine = 0, T.res[:, 16 * me:16 * me + 16]
+    for L, mask, w in ((offr, mo, 1), (onr, mn, 2)):
+        bl = bits(mask)
+        tr = []
+        for n, b in enumerate(L):
+            rid, pid = dst(cores[b])
+            tr.append(RemoteDMATransfer(dst_ids=[DstId(rid=rid, pnc=pid)], dma_engine_mask=sum(bl[w * n:w * n + w]),
+                                        remote_sem=S["resin"], srcs=[T.dres[b]], dsts=[mine], alu_op=0))
+            nres += w
+        g.remote_dma_fused(tr, local_sem=S["ressent"])
+    t_me = dma(Y, "y", mine, T.dres[me], "dd2", deps=td)
+    ss = T.ss
+    s1 = tt(ss[:, 0:96], T.res[:, 0:96], T.res[:, 96:192], OP.add, deps=[("resin", nres), t_me])
+    s2 = tt(ss[:, 96:144], ss[:, 0:48], ss[:, 48:96], OP.add, deps=[s1])
+    s3 = tt(ss[:, 144:160], ss[:, 96:112], ss[:, 112:128], OP.add, deps=[s2])
+    s4 = tt(ss[:, 160:176], ss[:, 144:160], ss[:, 128:144], OP.add, deps=[s3])
+    wait(P, "p", [s4, k_idf])
+    py = pt(P.transpose(T.ofp[0:16, 0:128], ss[:, 160:176], T.ident[:]))
+    ty = vcopy(T.ys[:], T.ofp[0:16, 0:128], deps=[py])
+    dma(Y, "y", T.y[0:12, :], T.ys[:, 0:96], "dy", deps=[ty])
+    dma(Y, "y", T.y[12:16, :], T.ys[:, 96:128], "dy")
+    wait(g, "g", [("dy", 32), ("rawsent", 16), ("psent", nsentp), ("ressent", nres), ("dta0", 16)])
+    wait(g, "g", [(k, cnt[k]) for k in ("v", "a", "p", "gp")])
+
+
+def slot_at_relay(cores, topo, d):
+    return [c for c in cores if topo.chip(c) == topo.chip(d)].index(d)

@@ -1,45 +1,47 @@
 from concourse.bass import DstId, RemoteDMATransfer
 from concourse.mybir import AluOpType as OP, ActivationFunctionType as AF
 
-NR, RC, CAP, H6, NC = 12, 8192, 512, 6, 96
+NR, RC, CAP = 12, 8192, 512
+LISTS = (7, 5)
+CM = 16 * LISTS[0]
 SLOTS = NR * CAP
-DUMP = 16 * NC
-WIN = SLOTS + DUMP
+WIN = SLOTS + 16 * CM
+OHW = 2 + NR * (CM + 2)
 
 SCRATCH = {
     "rawi": ("dram", [128, 16], "int32"), "rawj": ("dram", [128, 16], "int32"),
-    "rini": ("dram", [H6, 128, 16], "int32"), "rinj": ("dram", [H6, 128, 16], "int32"),
-    "dres": ("dram", [NR, 128, 16], "float32"),
+    "rini": ("dram", [LISTS[0], 128, 16], "int32"), "rinj": ("dram", [LISTS[0], 128, 16], "int32"),
+    "dres": ("dram", [NR, 128, 16], "float32"), "resd": ("dram", [NR, 128, 16], "float32"),
     "sta": ("sbuf", [128, RC], "float32"), "stb": ("sbuf", [128, RC], "float32"),
     "sb": ("sbuf", [128, SLOTS], "float32"), "rb": ("sbuf", [128, SLOTS], "float32"),
     "wa": ("sbuf", [128, WIN], "bfloat16"), "wb": ("sbuf", [128, WIN], "bfloat16"),
     "sw": ("sbuf", [128, WIN], "float32"),
-    "r0": ("sbuf", [128, DUMP], "float32"), "r1": ("sbuf", [128, DUMP], "float32"),
-    "va": ("sbuf", [128, DUMP], "bfloat16"), "vb": ("sbuf", [128, DUMP], "bfloat16"),
-    "oh": ("sbuf", [128, NR * NC], "bfloat16"), "onesb": ("sbuf", [128, NR * NC], "bfloat16"),
-    "ms": ("sbuf", [128, 576], "float32"), "t1": ("sbuf", [128, 576], "float32"), "t2": ("sbuf", [128, 288], "float32"),
+    "r0": ("sbuf", [128, 256 * LISTS[0]], "float32"), "r1": ("sbuf", [128, 256 * LISTS[1]], "float32"),
+    "va": ("sbuf", [128, 16 * CM], "bfloat16"), "vb": ("sbuf", [128, 16 * CM], "bfloat16"),
+    "oh": ("sbuf", [128, OHW], "bfloat16"), "maskb": ("sbuf", [128, 4 * (CM + 2)], "bfloat16"),
+    "pq": ("sbuf", [128, 3 * 512], "float32"),
     "prod": ("sbuf", [128, 2 * CAP], "float32"),
     "lb": ("sbuf", [128, 16 * 128], "bfloat16"), "zz": ("sbuf", [128, 16 * 132], "bfloat16"),
-    "li": ("sbuf", [128, NC], "int32"), "lj": ("sbuf", [128, NC], "int32"),
-    "i96": ("sbuf", [128, 6 * NC], "int32"), "b96": ("sbuf", [128, 6 * NC], "bfloat16"), "f96": ("sbuf", [128, 8 * NC], "float32"),
-    "ee": ("sbuf", [128, 16], "float32"), "e0": ("sbuf", [128, 12], "float32"), "tt": ("sbuf", [128, 12], "bfloat16"),
-    "base": ("sbuf", [128, 12], "float32"), "cb": ("sbuf", [128, 12], "float32"),
-    "sla": ("sbuf", [128, NC], "uint16"), "slb": ("sbuf", [128, NC], "uint16"), "slp": ("sbuf", [128, NC], "uint16"),
-    "xa": ("sbuf", [128, NC], "bfloat16"), "xb": ("sbuf", [128, NC], "bfloat16"),
-    "xpa": ("sbuf", [128, NC], "bfloat16"), "xpb": ("sbuf", [128, NC], "bfloat16"),
+    "li": ("sbuf", [128, CM], "int32"), "lj": ("sbuf", [128, CM], "int32"),
+    "i96": ("sbuf", [128, 6 * CM], "int32"), "b96": ("sbuf", [128, 6 * CM], "bfloat16"), "f96": ("sbuf", [128, 9 * CM], "float32"),
+    "sla": ("sbuf", [128, CM], "uint16"), "slb": ("sbuf", [128, CM], "uint16"),
+    "slt": ("sbuf", [128, CM], "uint16"), "slp": ("sbuf", [128, 16 * LISTS[1]], "uint16"),
+    "toff": ("sbuf", [128, 8 * LISTS[0]], "uint16"), "tof": ("sbuf", [128, 8 * LISTS[0]], "float32"),
+    "tl": ("sbuf", [128, 128 * LISTS[0]], "float32"), "bd": ("sbuf", [128, 128 * LISTS[0]], "bfloat16"),
+    "xa": ("sbuf", [128, 96], "bfloat16"), "xb": ("sbuf", [128, 96], "bfloat16"),
+    "xpa": ("sbuf", [128, 96], "bfloat16"), "xpb": ("sbuf", [128, 96], "bfloat16"), "xmb": ("sbuf", [128, 96], "bfloat16"),
     "offa": ("sbuf", [128, 384], "uint16"), "offb": ("sbuf", [128, 384], "uint16"),
-    "i16": ("sbuf", [128, 48], "int32"), "f16": ("sbuf", [128, 64], "float32"), "sel": ("sbuf", [128, 16], "bfloat16"),
-    "mask8": ("sbuf", [128, 8], "float32"),
+    "i16": ("sbuf", [128, 64], "int32"), "f16": ("sbuf", [128, 128], "float32"), "sel": ("sbuf", [128, 16], "bfloat16"),
     "i128": ("sbuf", [128, 256], "int32"), "mmf": ("sbuf", [128, 128], "float32"),
     "rep16": ("sbuf", [128, 128], "bfloat16"), "dd": ("sbuf", [128, 148], "float32"), "idz": ("sbuf", [128, 148], "bfloat16"),
-    "tri": ("sbuf", [128, 128], "bfloat16"), "ident": ("sbuf", [128, 128], "float32"), "onesf": ("sbuf", [128, 128], "float32"),
-    "res": ("sbuf", [128, NR * 16], "float32"), "ss": ("sbuf", [128, 192], "float32"), "ys": ("sbuf", [16, 128], "float32"),
+    "tri": ("sbuf", [128, 128], "bfloat16"), "trc": ("sbuf", [128, 128], "bfloat16"), "onesf": ("sbuf", [128, 128], "float32"),
+    "res": ("sbuf", [96, 256], "float32"), "ys": ("sbuf", [8, 256], "float32"),
     "cum": ("psum", [128, 1536], "float32"), "sc0": ("psum", [128, 512], "float32"), "sc1": ("psum", [128, 512], "float32"),
     "un": ("psum", [128, 512], "float32"), "sm": ("psum", [128, 512], "float32"), "ofp": ("psum", [128, 512], "float32"),
 }
-SEMAPHORES = (["v", "a", "p", "gp", "draw", "dself", "dl", "dl2", "dta0", "dta1", "dtb", "dd0", "dd1", "dd2", "dy",
-               "rawin", "rawsent", "xpa", "xpb", "slp", "xsent", "psent", "ressent", "resin", "rlsent"]
-              + ["pay%d" % k for k in range(NR)] + ["rl%d" % k for k in range(4)])
+SEMAPHORES = (["v", "a", "p", "gp", "draw", "dself", "dl", "dl2", "dta0", "dta1", "dtb", "dd0", "dd1", "dd2", "dx", "dy",
+               "rawin", "rawsent", "rawsent2", "xpa", "xpb", "xmb", "slp", "slm", "xsent", "psent", "ressent", "resin",
+               "rlsent"] + ["pay%d" % k for k in range(NR)] + ["rl%d" % k for k in range(4)])
 
 
 def bits(mask):
@@ -56,18 +58,20 @@ def plan(cores, topo):
         p = [d for d in range(ncore) if topo.chip(d) == topo.chip(c) and topo.die(d) == topo.die(c) and d not in taken][0]
         taken.add(p)
         partner[c] = p
+
+    def peer_index(s):
+        return [c for c in cores if topo.chip(c) == topo.chip(s) and topo.die(c) == topo.die(s)].index(s)
+
+    def mate_core(s, chip):
+        cand = [r for r in range(ncore) if topo.mates(topo.chip(r), chip) and topo.die(r) == topo.die(s)
+                and all(topo.may_write(r, e) for e in cores if topo.chip(e) == chip)]
+        return cand[peer_index(s) % len(cand)]
+
+    mate = {c: mate_core(c, topo.chip(c)) for c in cores}
     x, y = [(a, b) for a in chips for b in chips if a < b and topo.same_plane(a, b)][0]
     z = [c for c in chips if c not in (x, y)][0]
     relayed = {(y, x), (y, z), (z, y)}
-    relay = {}
-    for s in cores:
-        for d in cores:
-            if (topo.chip(s), topo.chip(d)) not in relayed:
-                continue
-            peers = [c for c in cores if topo.chip(c) == topo.chip(s) and topo.die(c) == topo.die(s)]
-            cand = [r for r in range(ncore) if topo.mates(topo.chip(r), topo.chip(d)) and topo.die(r) == topo.die(s)
-                    and all(topo.may_write(r, e) for e in cores if topo.chip(e) == topo.chip(d))]
-            relay[s, d] = cand[peers.index(s) % len(cand)]
+    relay = {(s, d): mate_core(s, topo.chip(d)) for s in cores for d in cores if (topo.chip(s), topo.chip(d)) in relayed}
     order = []
     for h in range(n):
         s = cores[h]
@@ -76,60 +80,52 @@ def plan(cores, topo):
         near = [b for b in range(n) if b != h and topo.chip(cores[b]) == topo.chip(s)]
         far = [L[h % 4:] + L[:h % 4] for L in far]
         near = near[h % 3:] + near[:h % 3]
-        o = []
-        for k in range(4):
-            o += [far[0][k], far[1][k]] + near[k:k + 1]
-        order.append(o + [h])
-    return partner, relay, order
+        f = [b for pair in zip(far[0], far[1]) for b in pair]
+        order.append([f[0], near[0], f[1], near[1], f[2], near[2]] + f[3:] + [h])
+    return partner, mate, relay, order
 
 
 def rank_program(g, core, T, topo):
     cores = list(T.cores)
-    partner, relay, order = plan(cores, topo)
-    owner_of = {p: c for c, p in partner.items()}
+    partner, mate, relay, order = plan(cores, topo)
     S = T.sem
     V, A, P, Y = g.vector, g.scalar, g.tensor, g.sync
     rank = T.rank_of(core)
+    role, own = None, core
+    if rank is not None:
+        role = "rank"
+    for c in cores:
+        if partner[c] == core:
+            role, own = "partner", c
+        if mate[c] == core:
+            role, own = "mate", c
+    if role is None:
+        return
+    me = cores.index(own)
+    is_owner = role == "rank"
+    up = role != "partner"
+    NL = LISTS[0] if up else LISTS[1]
+    NC = 16 * NL
+    NS, NB = NC + 2, 4 * (NC + 2)
+    cnt = {}
+    seen = {}
 
     def dst(c):
         rid, pid, _ = topo.addr(c)
         return rid, pid
 
-    if rank is None and core not in owner_of:
-        jobs = [(s, d) for (s, d), r in relay.items() if r == core]
-        if not jobs:
-            return
-        s = jobs[0][0]
-        h = cores.index(s)
-        jobs.sort(key=lambda sd: order[h].index(cores.index(sd[1])))
-        for _, d in jobs:
-            k = slot_at_relay(cores, topo, d)
-            g.wait_ge(S["rl%d" % k], 8)
-            rid, pid = dst(d)
-            g.remote_dma(out_ap=T.rb[:, CAP * h:CAP * h + CAP], in_ap=T.rb[:, CAP * k:CAP * k + CAP],
-                         remote_sem=S["pay%d" % h], local_sem=S["rlsent"], pid=pid, routing_id=rid,
-                         dma_engine_mask=topo.mask(core, d))
-        g.wait_ge(S["rlsent"], 8 * len(jobs))
-        return
-
-    own = core if rank is not None else owner_of[core]
-    me = cores.index(own)
-    half = 0 if rank is not None else 1
-    is_owner = half == 0
-    cnt = {}
-    seen = {}
-
-    def cut(buf, n, names):
-        return {name: buf[:, n * k:n * k + n] for k, name in enumerate(names)}
+    def cut(buf, stride, n, names):
+        return {name: buf[:, stride * k:stride * k + n] for k, name in enumerate(names)}
 
     B = {}
-    B.update(cut(T.i96, NC, ["hi", "hj", "xi", "xj", "xh", "xk"]))
-    B.update(cut(T.b96, NC, ["lo_a", "hi_a", "lo_b", "hi_b", "key", "keyb"]))
-    B.update(cut(T.f96, NC, ["tk", "nm", "dmp", "dump0", "dumpc", "t3", "t4", "t5"]))
-    B.update(cut(T.i16, 16, ["ip", "pm", "pg"]))
-    B.update(cut(T.f16, 16, ["pmf", "pgf", "ir", "mask16"]))
-    B.update(cut(T.i128, 128, ["im", "mm"]))
-    pcol = T.f16[:, 0:1]
+    B.update(cut(T.i96, CM, NC, ["hi", "hj", "xi", "xj", "xh", "xk"]))
+    B.update(cut(T.b96, CM, NC, ["lo_a", "hi_a", "lo_b", "hi_b", "key", "keyb"]))
+    B.update(cut(T.f96, CM, NC, ["tk", "nm", "dmp", "dump0", "dumpc", "t4", "t5", "kk", "dk"]))
+    B.update(cut(T.i16, 16, 16, ["ip", "pm", "pg", "p8"]))
+    B.update(cut(T.f16, 16, 16, ["pmf", "pgf", "ir", "mask16", "p8f", "mask8", "mask64", "seg8"]))
+    B.update(cut(T.i128, 128, 128, ["im", "mm"]))
+    pcol, gcol = T.f16[:, 0:1], T.f16[:, 16:17]
+    li, lj = T.li[:, 0:NC], T.lj[:, 0:NC]
 
     def wait(q, qn, deps):
         for t in deps:
@@ -178,79 +174,97 @@ def rank_program(g, core, T, topo):
         wait(P, "p", deps)
         return pt(P.matmul(out, lhsT, rhs, start, stop))
 
-    def act(out, in_, deps=()):
+    def act(out, in_, deps=(), **kw):
         wait(A, "a", deps)
-        return at(A.activation(out, in_, AF.Copy))
+        return at(A.activation(out, in_, AF.Copy, **kw))
 
-    tself = None
-    nraw = 8 * H6
+    tself = False
+    nraw = 8 * NL
+    first = LISTS[0]
     if is_owner:
-        ql, to = rank % H6, (cores if rank < H6 else [partner[c] for c in cores])
+        ql = rank if rank < first else rank - first
         dma(Y, "y", T.rawi[:], T.pi[:], "draw")
         dma(A, "a", T.rawj[:], T.pj[:], "draw")
-        if rank < H6:
+        if rank < first:
             dma(Y, "y", T.rini[ql], T.pi[:], "dself")
-            tself = dma(A, "a", T.rinj[ql], T.pj[:], "dself")
+            dma(A, "a", T.rinj[ql], T.pj[:], "dself")
             nraw -= 8
-        wait(g, "g", [("draw", 32)])
-        off = [c for c in to if topo.chip(c) != topo.chip(core)]
-        on = [c for c in to if topo.chip(c) == topo.chip(core) and c != core]
-        mo = topo.mask(core, off[0])
-        mn = topo.mask(core, on[0]) & ~mo
-        tr = []
-        for dl, mk_ in ((off, mo), (on, mn)):
-            b = bits(mk_)
-            ids = []
-            for c in dl:
-                rid, pid = dst(c)
-                ids.append(DstId(rid=rid, pnc=pid))
-            for src, buf, eng in ((T.rawi, T.rini, b[:4]), (T.rawj, T.rinj, b[4:8])):
-                tr.append(RemoteDMATransfer(dst_ids=ids, dma_engine_mask=sum(eng), remote_sem=S["rawin"],
-                                            srcs=[src[:]], dsts=[buf[ql] for _ in ids], alu_op=0))
-        g.remote_dma_fused(tr, local_sem=S["rawsent"])
-        dma(Y, "y", T.sta[:, 0:1024], T.ta[:, 0:1024], "dta0", deps=[("rawsent", 16)])
-
+            tself = True
     F = {"allow_small_or_imprecise_dtypes": True}
     c_ip = gt(g.iota(B["ip"], [[0, 16]], 0, 1))
     c_ir = gt(g.iota(B["ir"], [[1, 16]], 0, 0, **F))
     c_dd = gt(g.iota(T.dd[:], [[1, 148]], -1, -1, **F))
+    if is_owner:
+        offc = [c for c in cores if topo.chip(c) != topo.chip(core)]
+        mo = topo.mask(core, offc[0])
+        mn = topo.mask(core, partner[core]) & ~mo
+
+        def raw(parts, sem):
+            tr = []
+            for dl, mask in parts:
+                b = bits(mask)
+                ids = []
+                for c in dl:
+                    rid, pid = dst(c)
+                    ids.append(DstId(rid=rid, pnc=pid))
+                for src, buf, eng in ((T.rawi, T.rini, b[:4]), (T.rawj, T.rinj, b[4:8])):
+                    tr.append(RemoteDMATransfer(dst_ids=ids, dma_engine_mask=sum(eng), remote_sem=S["rawin"],
+                                                srcs=[src[:]], dsts=[buf[ql] for _ in ids], alu_op=0))
+            g.remote_dma_fused(tr, local_sem=S[sem])
+
+        to = [c for c in (cores if rank < first else [partner[c] for c in cores]) if c != core]
+        wait(g, "g", [("draw", 32)])
+        raw([([c for c in to if topo.chip(c) != topo.chip(core)], mo),
+             ([c for c in to if topo.chip(c) == topo.chip(core)], mn)], "rawsent")
+        if rank < first:
+            raw([([mate[c] for c in cores], mo)], "rawsent2")
+        dma(Y, "y", T.sta[:, 0:1024], T.ta[:, 0:1024], "dta0", deps=[("rawsent", 16)])
+
     c_du = gt(g.iota(B["dump0"], [[16, NC]], SLOTS, 0, **F))
-    c_cb = gt(g.iota(T.cb[:], [[CAP, 12]], -1 if is_owner else CAP, 0, **F))
     if is_owner:
         c_im = gt(g.iota(B["im"], [[1, 128]], 0, 0))
-    zwa = ms(T.wa[:, 0:SLOTS], 0.0)
-    k_ob = ms(T.onesb[:], 1.0)
-    k_ee = ms(T.ee[:], 0.0)
+    else:
+        c_to = gt(g.iota(T.tof[:, 0:8 * NL], [[16, NL], [0, 8]], 0, 0, **F))
+        c_bd = gt(g.iota(T.tl[:, 0:128 * NL], [[0, NL], [1, 8], [0, 16]], 0, 0, **F))
     k_pm = ts(B["pm"], B["ip"], 15, None, OP.bitwise_and, deps=[c_ip])
+    k_pg = ts(B["pg"], B["ip"], 4, None, OP.arith_shift_right)
     k_pmf = vcopy(B["pmf"], B["pm"], deps=[k_pm])
-    k_id = ts(T.idz[:], T.dd[:], 0.0, None, OP.is_equal, deps=[c_dd])
-    k_tri = ts(T.tri[:], T.dd[:, 1:129], 0.0, None, OP.is_gt)
+    k_pgf = vcopy(B["pgf"], B["pg"], deps=[k_pg])
     k_m16 = tt(B["mask16"], B["pmf"], B["ir"], OP.is_equal, deps=[k_pmf, c_ir])
+    k_id = ts(T.idz[:], T.dd[:], 0.0, None, OP.is_equal, deps=[c_dd])
     k_sel = tt(T.sel[:], B["pmf"], B["ir"], OP.is_equal)
-    k_du = ts(B["dumpc"], B["dump0"], pcol, None, OP.add, deps=[c_du])
     for r in range(16):
-        k_z = ts(T.zz[:, 132 * r:132 * r + 130], T.idz[:, r:r + 130], T.f16[:, 48 + r:49 + r], None, OP.mult,
-                 deps=[k_m16, k_id])
+        k_z = act(T.zz[:, 132 * r:132 * r + 130], T.idz[:, r:r + 130], deps=[k_m16, k_id], scale=T.f16[:, 48 + r:49 + r])
+    k_tri = ts(T.tri[:], T.dd[:, 1:129], 0.0, None, OP.is_gt)
+    k_trc = ts(T.trc[:], T.dd[:, 1:129], 0.0, None, OP.is_le)
+    k_oh = ms(T.oh[:], 0.0)
+    k_mb = ms(T.maskb[:, 0:NB], 1.0)
+    for c in range(4):
+        k_mb = ms(T.maskb[:, c * NS + 2:c * NS + 3], 0.0, deps=[k_mb])
+    k_du = ts(B["dumpc"], B["dump0"], pcol, None, OP.add, deps=[c_du, k_pmf])
+
+    def late_constants():
+        k1 = ts(T.toff[:, 0:8 * NL], T.tof[:, 0:8 * NL], pcol, None, OP.add, deps=[c_to])
+        k2 = ts(T.bd[:, 0:128 * NL], T.tl[:, 0:128 * NL], gcol, None, OP.is_equal, deps=[c_bd, k_pgf])
+        z = ms(T.wb[:, 0:SLOTS], 0.0)
+        return k1, k2, z
+
     if is_owner:
-        k_pg = ts(B["pg"], B["ip"], 4, None, OP.arith_shift_right)
         k_mm = ts(B["mm"], B["im"], 15, None, OP.bitwise_and, deps=[c_im])
-        k_pgf = vcopy(B["pgf"], B["pg"], deps=[k_pg])
+        k_m8 = tt(B["mask8"], B["pgf"], B["ir"], OP.is_equal, deps=[k_pgf])
         k_mmf = vcopy(T.mmf[:], B["mm"], deps=[k_mm])
-        k_m8 = tt(T.mask8[:], T.f16[:, 16:24], T.f16[:, 32:40], OP.is_equal, deps=[k_pgf])
+        k_m64 = ts(B["mask64"], B["mask8"], 64.0, None, OP.mult, deps=[k_m8])
         k_rep = ts(T.rep16[:], T.mmf[:], pcol, None, OP.is_equal, deps=[k_mmf])
-        for b in range(8):
-            for w in range(2):
-                k_lb = ts(T.lb[:, 128 * (2 * b + w):128 * (2 * b + w) + 128], T.rep16[:], T.mask8[:, b:b + 1],
-                          1.0 if w else 64.0, OP.mult, OP.mult, deps=[k_rep, k_m8])
-        k_of = ms(T.onesf[:], 1.0)
-        k_idf = ts(T.ident[:], T.dd[:, 1:129], 0.0, None, OP.is_equal)
+    if role == "mate":
+        k_to, k_bd, zwb = late_constants()
+    else:
+        zwa = ms(T.wa[:, 0:SLOTS], 0.0)
 
     for q, qn, src, out, sem in ((Y, "y", T.rini, T.li, "dl"), (A, "a", T.rinj, T.lj, "dl2")):
         wait(q, qn, [("rawin", nraw), ("dself", 32) if tself else None])
-        dma(q, qn, out[0:96, :], src[:, 0:96, :], sem)
-        for k in range(H6):
-            p0 = 96 + 16 * (k // 3)
-            dma(q, qn, out[p0:p0 + 16, 32 * (k % 3):32 * (k % 3) + 32], src[k, 96:128, :], sem)
+        dma(q, qn, out[0:NC, 0:NC], src[0:NL, 0:NC, :], sem)
+        for k in range(NL):
+            dma(q, qn, out[NC:128, 16 * k:16 * k + 16], src[k, NC:128, :], sem)
     l_i, l_j = ("dl", cnt["dl"]), ("dl2", cnt["dl2"])
     if is_owner:
         for a in range(1, 8):
@@ -258,17 +272,14 @@ def rank_program(g, core, T, topo):
         for a in range(4):
             t_tb = dma(Y, "y", T.stb[:, 2048 * a:2048 * a + 2048], T.tb[:, 2048 * a:2048 * a + 2048], "dtb")
 
-    ts(B["xi"], T.li[:], 63, None, OP.bitwise_and, deps=[l_i])
-    ts(B["xh"], T.li[:], 6, 127, OP.logical_shift_right, OP.bitwise_and)
-    b_hi = ts(B["hi"], T.li[:], 13, None, OP.logical_shift_right)
-    vcopy(B["lo_a"], B["xi"], deps=[b_hi])
-    b_ha = vcopy(B["hi_a"], B["xh"])
-    ts(B["hj"], T.lj[:], 13, None, OP.logical_shift_right, deps=[l_j])
-    b_t = ts(B["tk"], B["hi"], float(me), 16.0, OP.not_equal, OP.mult)
-    k_key = tt(B["key"], B["tk"], B["hj"], OP.add, deps=[b_t])
-
     banks = [T.sc0, T.sc1, T.un]
     bank_free = [None, None, None]
+
+    def places(l, x, xh, lo, hi):
+        ts(B[x], l, 63, None, OP.bitwise_and)
+        t = ts(B[xh], l, 6, 127, OP.logical_shift_right, OP.bitwise_and)
+        vcopy(B[lo], B[x], deps=[t])
+        return vcopy(B[hi], B[xh])
 
     def unwrap(lo, hi, out, blocks, dep):
         last = None
@@ -281,108 +292,166 @@ def rank_program(g, core, T, topo):
                 last = mm(o, T.zz[:, 132 * r:132 * r + 128], lo, False, True)
             for k in range(4):
                 r = 4 * blk + k
-                bank_free[blk % 3] = act(out[:, r:DUMP:16], bk[:, NC * k:NC * k + NC], deps=[last])
+                bank_free[blk % 3] = act(out[:, r:16 * NC:16], bk[:, NC * k:NC * k + NC], deps=[last])
         return bank_free[blocks[-1] % 3]
 
-    def rank1(key, dep, pdep):
-        nm = ts(B["nm"], key, 16.0, None, OP.is_ge, deps=[dep])
+    def one_hots(key, dep, pdep):
+        toks = []
         for c in range(NR):
-            o = ts(T.oh[:, NC * c:NC * c + NC], key, float(c), None, OP.is_equal, deps=[pdep])
-        dm = tt(B["dmp"], B["nm"], B["dumpc"], OP.mult, deps=[nm, k_du])
-        return o, dm
+            o = ts(T.oh[:, 4 + NS * c:4 + NS * c + NC], key, float(c), None, OP.is_equal, deps=[dep, k_oh])
+            if c % 4 == 3:
+                x = 2 + NB * (c // 4)
+                out = T.cum[:, 512 * (c // 4):512 * (c // 4) + NB]
+                mm(out, T.tri[:], T.oh[:, x:x + NB], True, False, deps=[o, k_tri, k_trc, pdep])
+                toks.append(mm(out, T.trc[:], T.oh[:, x - 1:x - 1 + NB], False, True))
+        nm = ts(B["nm"], key, 16.0, None, OP.is_ge)
+        kk = ts(B["kk"], key, float(CAP), 0.0 if up else float(CAP - 1), OP.mult, OP.add)
+        d = tt(B["dk"], B["dumpc"], B["kk"], OP.subtract, deps=[kk, k_du])
+        e = tt(B["dk"], B["nm"], B["dk"], OP.mult, deps=[d])
+        dm = tt(B["dmp"], B["dk"], B["kk"], OP.add, deps=[e])
+        return toks, dm
 
-    def rank2(o, dm, pdep):
-        wait(V, "v", [o, k_ob, k_ee])
-        s = vt(V.tensor_tensor_scan(T.cum[:, 0:NR * NC], T.onesb[:], T.oh[:], 0.0, OP.mult,
-                                    OP.add if is_owner else OP.subtract))
-        e = vcopy(T.ee[:, 1:13], T.cum[:, NC - 1:NR * NC:NC], deps=[s])
-        t = tt(T.tt[:], T.ee[:, 1:13], T.ee[:, 0:12], OP.subtract, deps=[e])
-        e0 = tt(T.e0[:], T.ee[:, 0:12], T.cb[:], OP.subtract, deps=[c_cb])
-        m = mm(T.sm[:, 0:12], T.tri[:], T.tt[:], deps=[t, k_tri, pdep])
-        return e0, m
-
-    def rank3(e0, m, dm, sl):
-        b = tt(T.base[:], T.sm[:, 0:12], T.e0[:], OP.subtract, deps=[m, e0])
-        for c in range(NR):
-            o = ts(T.cum[:, NC * c:NC * c + NC], T.cum[:, NC * c:NC * c + NC], T.base[:, c:c + 1], None, OP.add, deps=[b])
-        tt(T.ms[:], T.cum[:, 576:1152], T.oh[:, 576:1152], OP.mult, deps=[o])
-        m1 = tt(T.cum[:, 0:576], T.cum[:, 0:576], T.oh[:, 0:576], OP.mult)
-        a1 = tt(T.t1[:], T.cum[:, 0:576], T.ms[:], OP.add, deps=[m1])
-        a2 = tt(T.t2[:], T.t1[:, 0:288], T.t1[:, 288:576], OP.add, deps=[a1])
-        tt(B["t3"], T.t2[:, 0:96], T.t2[:, 96:192], OP.add, deps=[a2])
-        a4 = tt(B["t4"], T.t2[:, 192:288], B["dmp"], OP.add, deps=[dm])
-        a5 = tt(B["t5"], B["t3"], B["t4"], OP.add, deps=[a4])
-        return vcopy(sl[:], B["t5"], deps=[a5])
+    def slots(toks, dm, sl):
+        pq = T.pq
+        m = []
+        for k in range(3):
+            o = (T.ofp, T.sm, T.ofp)[k][:, 0:NB]
+            c = T.cum[:, 512 * k:512 * k + NB]
+            wait(V, "v", [toks[k], k_mb, ("v", cnt["v"])])
+            s = vt(V.tensor_tensor_scan(o, T.maskb[:, 0:NB], c, 0.0, OP.mult, OP.add))
+            m.append(tt(pq[:, 0:NB] if k == 1 else c, o, T.oh[:, 2 + NB * k:2 + NB * k + NB], OP.mult, deps=[s]))
+        a1 = tt(pq[:, 512:512 + NB], T.cum[:, 0:NB], pq[:, 0:NB], OP.add, deps=[m[1]])
+        a2 = tt(pq[:, 1024:1024 + NB], T.cum[:, 1024:1024 + NB], pq[:, 512:512 + NB], OP.add, deps=[a1, m[2]])
+        a3 = tt(pq[:, 0:2 * NS], pq[:, 1024:1024 + 2 * NS], pq[:, 1024 + 2 * NS:1024 + NB], OP.add, deps=[a2])
+        a4 = tt(B["t4"], pq[:, 2:NS], pq[:, NS + 2:2 * NS], OP.add, deps=[a3])
+        a5 = tt(B["t5"], B["dmp"], B["t4"], OP.add if up else OP.subtract, deps=[a4, dm])
+        return vcopy(sl[:, 0:NC], B["t5"], deps=[a5])
 
     def scatter(win, sl, vals, deps):
         wait(V, "v", deps)
-        return vt(V.tensor_copy(win[:, 0:WIN].indirect(sl[:, 0:NC]), vals[:]))
+        return vt(V.tensor_copy(win[:, 0:SLOTS + 16 * NC].indirect(sl[:, 0:NC]), vals[:, 0:16 * NC]))
 
-    def wrap1(win, dep, free):
+    def wrap1(win, dep):
         for ch in range(48):
-            t = mm(T.sm[:, 32 + 2 * ch:34 + 2 * ch], win[:, 128 * ch:128 * ch + 128], T.sel[:, 0:2], deps=[dep, k_sel, free])
+            t = mm(T.sm[:, 2 * ch:2 * ch + 2], win[:, 128 * ch:128 * ch + 128], T.sel[:, 0:2], deps=[dep, k_sel])
         return t
 
-    def wrap2(x, dep, free):
+    def wrap2(x, dep):
         for b in range(8):
             o = T.ofp[:, b:384:8]
-            mm(o, T.lb[:, 256 * b:256 * b + 128], x[:, 0:NC:2], True, False, deps=[dep, k_lb, free])
-            t = mm(o, T.lb[:, 256 * b + 128:256 * b + 256], x[:, 1:NC:2], False, True)
+            mm(o, T.lb[:, 256 * b:256 * b + 128], x[:, 0:96:2], True, False, deps=[dep, k_lb])
+            t = mm(o, T.lb[:, 256 * b + 128:256 * b + 256], x[:, 1:96:2], False, True)
         return t
 
-    unwrap(B["lo_a"], B["hi_a"], T.va, [0, 1, 2], b_ha)
-    o, dm = rank1(B["key"], k_key, None)
-    e0, m = rank2(o, dm, None)
-    u_a = unwrap(B["lo_a"], B["hi_a"], T.va, [3], b_ha)
-    ts(B["xj"], T.lj[:], 63, None, OP.bitwise_and)
-    b_hk = ts(B["xk"], T.lj[:], 6, 127, OP.logical_shift_right, OP.bitwise_and)
-    vcopy(B["lo_b"], B["xj"], deps=[b_hk])
-    b_hb = vcopy(B["hi_b"], B["xk"])
-    sl_a = rank3(e0, m, dm, T.sla)
-    u_b = unwrap(B["lo_b"], B["hi_b"], T.vb, [0, 1, 2, 3], b_hb)
-    sc_a = scatter(T.wa, T.sla, T.va, [sl_a, u_a, zwa])
-    w_a = wrap1(T.wa, sc_a, None)
-    zwb = ms(T.wb[:, 0:SLOTS], 0.0)
-    b_t = ts(B["tk"], B["hj"], float(me), 16.0, OP.not_equal, OP.mult)
-    k_kb = tt(B["keyb"], B["tk"], B["hi"], OP.add, deps=[b_t])
+    def turn(dep):
+        f5 = T.f96[:, 6 * CM:6 * CM + NC]
+        wait(V, "v", [dep, k_to, k_bd])
+        t = vt(V.tensor_copy(T.tl[:, 0:128 * NL], f5.indirect(T.toff[:, 0:8 * NL])))
+        t = tt(T.tl[:, 0:128 * NL], T.tl[:, 0:128 * NL], T.bd[:, 0:128 * NL], OP.mult, deps=[t])
+        for c in range(NL):
+            mm(T.un[:, c:NC:NL], T.tl[:, 128 * c:128 * c + 128], B["mask16"], deps=[t, u_b])
+            p = mm(T.un[:, 128 + 16 * c:144 + 16 * c], T.tl[:, 128 * c:128 * c + 128], B["mask16"])
+        t = vcopy(T.slt[:, 0:NC], T.un[:, 128:128 + NC], deps=[p])
+        return vcopy(T.slt[0:NC, 0:NC], T.un[0:NC, 0:NC], deps=[t])
 
-    if not is_owner:
-        x_a = vcopy(T.xa[:], T.sm[:, 32:128], deps=[w_a])
+    def send(out, src, name, dep):
         rid, pid = dst(own)
+        mask = topo.mask(core, own)
+        wait(g, "g", [dep])
+        g.remote_dma(out_ap=out, in_ap=src, remote_sem=S[name], local_sem=S["xsent"], pid=pid, routing_id=rid,
+                     dma_engine_mask=mask)
+        return len(bits(mask))
 
-        def send(buf, src, name, dep):
-            wait(g, "g", [dep])
-            g.remote_dma(out_ap=buf[:], in_ap=src[:], remote_sem=S[name], local_sem=S["xsent"], pid=pid,
-                         routing_id=rid, dma_engine_mask=topo.mask(core, own))
-
-        send(T.xpa, T.xa, "xpa", x_a)
-        o, dm = rank1(B["keyb"], k_kb, None)
-        e0, m = rank2(o, dm, x_a)
-        sl_b = rank3(e0, m, dm, T.slb)
+    if role == "mate":
+        b_hj = ts(B["hj"], lj, 13, None, OP.logical_shift_right, deps=[l_j])
+        b_hb = places(lj, "xj", "xk", "lo_b", "hi_b")
+        ts(B["tk"], B["hj"], float(me), 16.0, OP.not_equal, OP.mult)
+        b_hi = ts(B["hi"], li, 13, None, OP.logical_shift_right, deps=[l_i])
+        k_kb = tt(B["keyb"], B["tk"], B["hi"], OP.add, deps=[b_hi])
+        unwrap(B["lo_b"], B["hi_b"], T.vb, [0, 1], b_hb)
+        toks, dm = one_hots(B["keyb"], k_kb, None)
+        u_b = unwrap(B["lo_b"], B["hi_b"], T.vb, [2, 3], b_hb)
+        sl_b = slots(toks, dm, T.slb)
         sc_b = scatter(T.wb, T.slb, T.vb, [sl_b, u_b, zwb])
-        w_b = wrap1(T.wb, sc_b, None)
-        x_b = vcopy(T.xb[:], T.sm[:, 32:128], deps=[w_b])
-        send(T.xpb, T.xb, "xpb", x_b)
-        send(T.slp, T.slb, "slp", sl_b)
+        w_b = wrap1(T.wb, sc_b)
+        x_b = vcopy(T.xb[:], T.sm[:, 0:96], deps=[w_b])
+        n = send(T.xmb[:], T.xb[:], "xmb", x_b)
+        n += send(T.slt[:], T.slt[:], "slm", turn(sl_b))
+        jobs = [(s, d) for (s, d), r in relay.items() if r == core]
+        for s, d in sorted(jobs, key=lambda sd: order[cores.index(sd[0])].index(cores.index(sd[1]))):
+            h, k = cores.index(s), slot_at_relay(cores, topo, d)
+            g.wait_ge(S["rl%d" % k], 8)
+            rid, pid = dst(d)
+            g.remote_dma(out_ap=T.rb[:, CAP * h:CAP * h + CAP], in_ap=T.rb[:, CAP * k:CAP * k + CAP],
+                         remote_sem=S["pay%d" % h], local_sem=S["rlsent"], pid=pid, routing_id=rid,
+                         dma_engine_mask=topo.mask(core, d))
+        wait(g, "g", [("rlsent", 8 * len(jobs)) if jobs else None, ("xsent", n)])
         wait(g, "g", [(k, cnt[k]) for k in ("v", "a", "p", "gp")])
-        wait(g, "g", [("xsent", 48)])
         return
 
-    o, dm = rank1(B["keyb"], k_kb, None)
-    x_a = tt(T.xa[:], T.sm[:, 32:128], T.xpa[:], OP.add, deps=[w_a, ("xpa", 16)])
-    p_a = wrap2(T.xa, x_a, None)
-    e0, m = rank2(o, dm, x_a)
+    b_hi = ts(B["hi"], li, 13, None, OP.logical_shift_right, deps=[l_i])
+    b_ha = places(li, "xi", "xh", "lo_a", "hi_a")
+    ts(B["tk"], B["hi"], float(me), 16.0, OP.not_equal, OP.mult)
+    b_hj = ts(B["hj"], lj, 13, None, OP.logical_shift_right, deps=[l_j])
+    k_key = tt(B["key"], B["tk"], B["hj"], OP.add, deps=[b_hj])
+    unwrap(B["lo_a"], B["hi_a"], T.va, [0, 1], b_ha)
+    toks, dm = one_hots(B["key"], k_key, None)
+    u_a = unwrap(B["lo_a"], B["hi_a"], T.va, [2, 3], b_ha)
+    sl_a = slots(toks, dm, T.sla)
+
+    if role == "partner":
+        b_hb = places(lj, "xj", "xk", "lo_b", "hi_b")
+        u_b = unwrap(B["lo_b"], B["hi_b"], T.vb, [0, 1, 2, 3], b_hb)
+        sc_a = scatter(T.wa, T.sla, T.va, [sl_a, u_a, zwa])
+        w_a = wrap1(T.wa, sc_a)
+        b_t = ts(B["tk"], B["hj"], float(me), 16.0, OP.not_equal, OP.mult)
+        k_kb = tt(B["keyb"], B["tk"], B["hi"], OP.add, deps=[b_t])
+        toks, dm = one_hots(B["keyb"], k_kb, sl_a)
+        x_a = vcopy(T.xa[:], T.sm[:, 0:96], deps=[w_a])
+        n = send(T.xpa[:], T.xa[:], "xpa", x_a)
+        k_to, k_bd, zwb = late_constants()
+        sl_b = slots(toks, dm, T.slb)
+        sc_b = scatter(T.wb, T.slb, T.vb, [sl_b, u_b, zwb])
+        w_b = wrap1(T.wb, sc_b)
+        x_b = vcopy(T.xb[:], T.sm[:, 0:96], deps=[w_b])
+        n += send(T.xpb[:], T.xb[:], "xpb", x_b)
+        n += send(T.slp[:], T.slt[:, 0:NC], "slp", turn(sl_b))
+        wait(g, "g", [("xsent", n)])
+        wait(g, "g", [(k, cnt[k]) for k in ("v", "a", "p", "gp")])
+        return
+
+    sc_a = scatter(T.wa, T.sla, T.va, [sl_a, u_a, zwa])
+    w_a = wrap1(T.wa, sc_a)
+    for b in range(8):
+        for w in range(2):
+            c = (80 if w else 96) + b
+            k_lb = act(T.lb[:, 128 * (2 * b + w):128 * (2 * b + w) + 128], T.rep16[:], deps=[k_rep, k_m64],
+                       scale=T.f16[:, c:c + 1])
+    k_of = ms(T.onesf[:], 1.0)
+    k_p8 = ts(B["p8"], B["ip"], 7, None, OP.bitwise_and)
+    zsw = ms(T.sw[:, SLOTS:WIN], 0.0)
+    k_p8f = vcopy(B["p8f"], B["p8"], deps=[k_p8])
+    k_seg = tt(B["seg8"], B["p8f"], B["ir"], OP.is_equal, deps=[k_p8f])
+    np = len(bits(topo.mask(partner[core], core)))
+    nm_ = len(bits(topo.mask(mate[core], core)))
+    x_a = tt(T.xa[:], T.sm[:, 0:96], T.xpa[:], OP.add, deps=[w_a, ("xpa", np)])
+    p_a = wrap2(T.xa, x_a)
     o_a = vcopy(T.offa[:], T.ofp[:, 0:384], deps=[p_a])
 
     full = {}
     nsentp = 0
     for b in order[me]:
-        tg = act(T.sb[:, CAP * b:CAP * b + CAP], T.sta[:, 0:RC].indirect(T.offa[:, 32 * b:32 * b + 32]),
-                 deps=[o_a, ("dta0", 16), t_ta])
+        d = cores[b]
+        src = T.sta[:, 0:RC].indirect(T.offa[:, 32 * b:32 * b + 32])
+        blk = T.sb[:, CAP * b:CAP * b + CAP]
+        deps = [o_a, ("dta0", 16), t_ta]
+        if topo.chip(d) == topo.chip(core):
+            tg = vcopy(blk, src, deps=deps)
+        else:
+            tg = act(blk, src, deps=deps)
         full[b] = tg
         if b == me:
             continue
-        d = cores[b]
         wait(g, "g", [tg])
         if (core, d) in relay:
             to = relay[core, d]
@@ -395,27 +464,26 @@ def rank_program(g, core, T, topo):
         if topo.chip(to) == topo.chip(core):
             mask &= ~mo
         rid, pid = dst(to)
-        g.remote_dma(out_ap=out, in_ap=T.sb[:, CAP * b:CAP * b + CAP], remote_sem=S[sem], local_sem=S["psent"],
-                     pid=pid, routing_id=rid, dma_engine_mask=mask)
+        g.remote_dma(out_ap=out, in_ap=blk, remote_sem=S[sem], local_sem=S["psent"], pid=pid, routing_id=rid,
+                     dma_engine_mask=mask)
         nsentp += 8
 
-    sl_b = rank3(e0, m, dm, T.slb)
-    sc_b = scatter(T.wb, T.slb, T.vb, [sl_b, u_b, zwb])
-    w_b = wrap1(T.wb, sc_b, None)
-    zsw = ms(T.sw[:, SLOTS:WIN], 0.0)
-    x_b = tt(T.xb[:], T.sm[:, 32:128], T.xpb[:], OP.add, deps=[w_b, ("xpb", 16)])
-    p_b = wrap2(T.xb, x_b, o_a)
+    x_b = tt(T.xb[:], T.xpb[:], T.xmb[:], OP.add, deps=[("xpb", np), ("xmb", nm_)])
+    p_b = wrap2(T.xb, x_b)
     o_b = vcopy(T.offb[:], T.ofp[:, 0:384], deps=[p_b])
 
     def arrival(h):
         if h == me:
-            return 0
-        return order[h].index(me) + (3 if (cores[h], core) in relay else 0)
+            return 2.0
+        same = topo.chip(cores[h]) == topo.chip(core)
+        row = [b for b in order[h] if (topo.chip(cores[b]) == topo.chip(cores[h])) == same]
+        return row.index(me) + 1.0 + (2.5 if (cores[h], core) in relay else 0.0)
 
-    scs = [T.sc0, T.sc1]
-    pm_, pc_ = [None, None], [u_b, u_b]
+    scs = [T.sc0[:], T.sc1[:], T.un[:]] + [T.cum[:, 512 * k:512 * k + 512] for k in range(3)]
+    pm_ = [None, None]
+    pc_ = [u_a, u_a, u_a, sl_a, sl_a, sl_a]
     for n, h in enumerate(sorted(range(NR), key=lambda h: (arrival(h), h))):
-        k = n % 2
+        k, j = n % 2, n % 6
         pr = T.prod[:, CAP * k:CAP * k + CAP]
         blk = T.rb
         if h == me:
@@ -423,44 +491,41 @@ def rank_program(g, core, T, topo):
         wait(V, "v", [o_b, t_tb, full[me] if h == me else ("pay%d" % h, 8), pm_[k]])
         t = vt(V.tensor_tensor(pr, T.stb[:, 0:RC].indirect(T.offb[:, 32 * h:32 * h + 32]),
                                blk[:, CAP * h:CAP * h + CAP], OP.mult))
-        pm_[k] = mm(scs[k][:], T.onesf[:], pr, deps=[t, k_of, pc_[k]])
-        pc_[k] = act(T.sw[:, CAP * h:CAP * h + CAP], scs[k][:], deps=[pm_[k]])
+        pm_[k] = mm(scs[j], T.onesf[:], pr, deps=[t, k_of, pc_[j]])
+        pc_[j] = act(T.sw[:, CAP * h:CAP * h + CAP], scs[j], deps=[pm_[k]])
 
-    wait(V, "v", [pc_[0], pc_[1], zsw, sl_b])
-    f0 = vt(V.tensor_copy(T.r0[:], T.sw[:, 0:WIN].indirect(T.slb[:, 0:NC])))
-    wait(A, "a", [pc_[0], pc_[1], zsw, ("slp", 16)])
-    f1 = at(A.activation(T.r1[:], T.sw[:, 0:WIN].indirect(T.slp[:, 0:NC]), AF.Copy))
-    for q, qn, R, f, sem, d0 in ((Y, "y", T.r0, f0, "dd0", 0), (A, "a", T.r1, f1, "dd1", H6)):
+    wait(V, "v", pc_ + [zsw, ("slm", nm_)])
+    f0 = vt(V.tensor_copy(T.r0[:], T.sw[:, 0:WIN].indirect(T.slt[:, 0:NC])))
+    wait(A, "a", pc_ + [zsw, ("slp", np)])
+    f1 = at(A.activation(T.r1[:], T.sw[:, 0:WIN].indirect(T.slp[:]), AF.Copy))
+    d0 = 0
+    for q, qn, R, f, sem, n in ((Y, "y", T.r0, f0, "dd0", LISTS[0]), (A, "a", T.r1, f1, "dd1", LISTS[1])):
         wait(q, qn, [f])
-        dma(q, qn, T.dres[d0:d0 + 6, 0:96, :], R[0:96:16, :], sem)
-        dma(q, qn, T.dres[d0:d0 + 3, 96:128, :], R[96:97, :], sem)
-        dma(q, qn, T.dres[d0 + 3:d0 + 6, 96:128, :], R[112:113, :], sem)
-    td = [("dd0", 48), ("dd1", 48)]
+        dma(q, qn, T.dres[d0:d0 + n, 0:16 * n, :], R[0:16 * n:16, :], sem)
+        for p in range(16 * n, 128, 16):
+            dma(q, qn, T.dres[d0:d0 + n, p:p + 16, :], R[p:p + 1, :], sem)
+        d0 += n
+    td = [("dd0", cnt["dd0"]), ("dd1", cnt["dd1"])]
     wait(g, "g", td)
     offr = [b for b in range(NR) if topo.chip(cores[b]) != topo.chip(core)]
     onr = [b for b in range(NR) if topo.chip(cores[b]) == topo.chip(core) and b != me]
-    nres, mine = 0, T.res[:, 16 * me:16 * me + 16]
+    nres = 0
     for L, mask, w in ((offr, mo, 1), (onr, mn, 2)):
         bl = bits(mask)
         tr = []
         for n, b in enumerate(L):
             rid, pid = dst(cores[b])
             tr.append(RemoteDMATransfer(dst_ids=[DstId(rid=rid, pnc=pid)], dma_engine_mask=sum(bl[w * n:w * n + w]),
-                                        remote_sem=S["resin"], srcs=[T.dres[b]], dsts=[mine], alu_op=0))
+                                        remote_sem=S["resin"], srcs=[T.dres[b]], dsts=[T.resd[me]], alu_op=0))
             nres += w
         g.remote_dma_fused(tr, local_sem=S["ressent"])
-    t_me = dma(Y, "y", mine, T.dres[me], "dd2", deps=td)
-    ss = T.ss
-    s1 = tt(ss[:, 0:96], T.res[:, 0:96], T.res[:, 96:192], OP.add, deps=[("resin", nres), t_me])
-    s2 = tt(ss[:, 96:144], ss[:, 0:48], ss[:, 48:96], OP.add, deps=[s1])
-    s3 = tt(ss[:, 144:160], ss[:, 96:112], ss[:, 112:128], OP.add, deps=[s2])
-    s4 = tt(ss[:, 160:176], ss[:, 144:160], ss[:, 128:144], OP.add, deps=[s3])
-    wait(P, "p", [s4, k_idf])
-    py = pt(P.transpose(T.ofp[0:16, 0:128], ss[:, 160:176], T.ident[:]))
-    ty = vcopy(T.ys[:], T.ofp[0:16, 0:128], deps=[py])
-    dma(Y, "y", T.y[0:12, :], T.ys[:, 0:96], "dy", deps=[ty])
-    dma(Y, "y", T.y[12:16, :], T.ys[:, 96:128], "dy")
-    wait(g, "g", [("dy", 32), ("rawsent", 16), ("psent", nsentp), ("ressent", nres), ("dta0", 16)])
+    t_me = dma(Y, "y", T.resd[me], T.dres[me], "dd2", deps=td)
+    t_x = dma(Y, "y", T.res[:], T.resd[:], "dx", deps=[t_me, ("resin", nres)])
+    py = mm(T.ofp[0:8, 0:256], T.f16[0:96, 112:120], T.res[:], deps=[t_x, k_seg])
+    ty = vcopy(T.ys[:], T.ofp[0:8, 0:256], deps=[py])
+    dma(Y, "y", T.y[:], T.ys[:], "dy", deps=[ty])
+    wait(g, "g", [("dy", 16), ("rawsent", 16), ("psent", nsentp), ("ressent", nres), ("dta0", 16),
+                  ("rawsent2", 8) if rank < first else None])
     wait(g, "g", [(k, cnt[k]) for k in ("v", "a", "p", "gp")])
 
 

@@ -3,45 +3,51 @@ from concourse.mybir import AluOpType as OP, ActivationFunctionType as AF
 
 NR, RC, CAP = 12, 8192, 512
 LISTS = (7, 5)
-CM = 16 * LISTS[0]
+CM = 16 * max(LISTS)
 SLOTS = NR * CAP
 WIN = SLOTS + 16 * CM
 OHW = 2 + NR * (CM + 2)
+PA = 4
+WINDOW = 3
+NE = 4
+EL = 2
 
 SCRATCH = {
     "rawi": ("dram", [128, 16], "int32"), "rawj": ("dram", [128, 16], "int32"),
-    "rini": ("dram", [LISTS[0], 128, 16], "int32"), "rinj": ("dram", [LISTS[0], 128, 16], "int32"),
+    "rini": ("dram", [CM // 16, 128, 16], "int32"), "rinj": ("dram", [CM // 16, 128, 16], "int32"),
     "dres": ("dram", [NR, 128, 16], "float32"), "resd": ("dram", [NR, 128, 16], "float32"),
     "sta": ("sbuf", [128, RC], "float32"), "stb": ("sbuf", [128, RC], "float32"),
     "sb": ("sbuf", [128, SLOTS], "float32"), "rb": ("sbuf", [128, SLOTS], "float32"),
-    "wa": ("sbuf", [128, WIN], "bfloat16"), "wb": ("sbuf", [128, WIN], "bfloat16"),
+    "wa": ("sbuf", [128, WIN], "bfloat16"),
     "sw": ("sbuf", [128, WIN], "float32"),
     "r0": ("sbuf", [128, 256 * LISTS[0]], "float32"), "r1": ("sbuf", [128, 256 * LISTS[1]], "float32"),
-    "va": ("sbuf", [128, 16 * CM], "bfloat16"), "vb": ("sbuf", [128, 16 * CM], "bfloat16"),
+    "va": ("sbuf", [128, 16 * CM], "bfloat16"),
     "oh": ("sbuf", [128, OHW], "bfloat16"), "maskb": ("sbuf", [128, 4 * (CM + 2)], "bfloat16"),
-    "pq": ("sbuf", [128, 3 * 512], "float32"),
+    "xq": ("sbuf", [128, 12 * (CM + 2)], "float16"),
     "prod": ("sbuf", [128, 2 * CAP], "float32"),
     "lb": ("sbuf", [128, 16 * 128], "bfloat16"), "zz": ("sbuf", [128, 16 * 132], "bfloat16"),
-    "li": ("sbuf", [128, CM], "int32"), "lj": ("sbuf", [128, CM], "int32"),
-    "i96": ("sbuf", [128, 6 * CM], "int32"), "b96": ("sbuf", [128, 6 * CM], "bfloat16"), "f96": ("sbuf", [128, 9 * CM], "float32"),
-    "sla": ("sbuf", [128, CM], "uint16"), "slb": ("sbuf", [128, CM], "uint16"),
-    "slt": ("sbuf", [128, CM], "uint16"), "slp": ("sbuf", [128, 16 * LISTS[1]], "uint16"),
-    "toff": ("sbuf", [128, 8 * LISTS[0]], "uint16"), "tof": ("sbuf", [128, 8 * LISTS[0]], "float32"),
-    "tl": ("sbuf", [128, 128 * LISTS[0]], "float32"), "bd": ("sbuf", [128, 128 * LISTS[0]], "bfloat16"),
+    "lij": ("sbuf", [128, 2 * CM], "int32"), "h96": ("sbuf", [128, 2 * CM], "int32"),
+    "i96": ("sbuf", [128, 2 * CM], "int32"), "b96": ("sbuf", [128, 3 * CM], "bfloat16"), "f96": ("sbuf", [128, 5 * CM], "float32"),
+    "sla": ("sbuf", [128, CM], "uint16"),
+    "slt": ("sbuf", [128, CM], "uint16"), "slp": ("sbuf", [128, CM], "uint16"),
+    "toff": ("sbuf", [128, CM // 2], "uint16"), "tof": ("sbuf", [128, CM // 2], "float32"),
+    "tl": ("sbuf", [128, 8 * CM], "float32"), "bd": ("sbuf", [128, 8 * CM], "bfloat16"),
     "xa": ("sbuf", [128, 96], "bfloat16"), "xb": ("sbuf", [128, 96], "bfloat16"),
     "xpa": ("sbuf", [128, 96], "bfloat16"), "xpb": ("sbuf", [128, 96], "bfloat16"), "xmb": ("sbuf", [128, 96], "bfloat16"),
     "offa": ("sbuf", [128, 384], "uint16"), "offb": ("sbuf", [128, 384], "uint16"),
     "i16": ("sbuf", [128, 64], "int32"), "f16": ("sbuf", [128, 128], "float32"), "sel": ("sbuf", [128, 16], "bfloat16"),
     "i128": ("sbuf", [128, 256], "int32"), "mmf": ("sbuf", [128, 128], "float32"),
     "rep16": ("sbuf", [128, 128], "bfloat16"), "dd": ("sbuf", [128, 148], "float32"), "idz": ("sbuf", [128, 148], "bfloat16"),
+    "idf": ("sbuf", [128, 128], "float32"), "idh": ("sbuf", [128, 128], "float16"), "id5": ("sbuf", [128, 128], "bfloat16"),
     "tri": ("sbuf", [128, 128], "bfloat16"), "trc": ("sbuf", [128, 128], "bfloat16"), "onesf": ("sbuf", [128, 128], "float32"),
     "res": ("sbuf", [96, 256], "float32"), "ys": ("sbuf", [8, 256], "float32"),
     "cum": ("psum", [128, 1536], "float32"), "sc0": ("psum", [128, 512], "float32"), "sc1": ("psum", [128, 512], "float32"),
     "un": ("psum", [128, 512], "float32"), "sm": ("psum", [128, 512], "float32"), "ofp": ("psum", [128, 512], "float32"),
 }
 SEMAPHORES = (["v", "a", "p", "gp", "draw", "dself", "dl", "dl2", "dta0", "dta1", "dtb", "dd0", "dd1", "dd2", "dx", "dy",
-               "rawin", "rawsent", "rawsent2", "xpa", "xpb", "xmb", "slp", "slm", "xsent", "psent", "ressent", "resin",
-               "rlsent"] + ["pay%d" % k for k in range(NR)] + ["rl%d" % k for k in range(4)])
+               "rawin", "rawsent", "rawsent2", "xpa", "xpa2", "xpb", "xmb", "xpb2", "xmb2", "slp", "slm", "xsent", "psent",
+               "ressent", "resin", "rlsent"] + ["pay%d" % k for k in range(NR)] + ["ps%d" % k for k in range(8)]
+              + ["rl%d" % k for k in range(4)])
 
 
 def bits(mask):
@@ -68,6 +74,13 @@ def plan(cores, topo):
         return cand[peer_index(s) % len(cand)]
 
     mate = {c: mate_core(c, topo.chip(c)) for c in cores}
+    helper = {}
+    for c in cores:
+        free = [d for d in range(ncore) if topo.same_plane(topo.chip(d), topo.chip(c)) and topo.die(d) == topo.die(c)
+                and topo.chip(d) not in chips and not any(topo.mates(topo.chip(d), x) for x in chips) and d not in taken]
+        p = min(free, key=lambda d: (sum(topo.chip(t) == topo.chip(d) for t in helper.values()), d))
+        taken.add(p)
+        helper[c] = p
     x, y = [(a, b) for a in chips for b in chips if a < b and topo.same_plane(a, b)][0]
     z = [c for c in chips if c not in (x, y)][0]
     relayed = {(y, x), (y, z), (z, y)}
@@ -81,13 +94,13 @@ def plan(cores, topo):
         far = [L[h % 4:] + L[:h % 4] for L in far]
         near = near[h % 3:] + near[:h % 3]
         f = [b for pair in zip(far[0], far[1]) for b in pair]
-        order.append([f[0], near[0], f[1], near[1], f[2], near[2]] + f[3:] + [h])
-    return partner, mate, relay, order
+        order.append(f[:3] + near + f[3:4] + [h] + f[4:])
+    return partner, mate, helper, relay, order
 
 
 def rank_program(g, core, T, topo):
     cores = list(T.cores)
-    partner, mate, relay, order = plan(cores, topo)
+    partner, mate, helper, relay, order = plan(cores, topo)
     S = T.sem
     V, A, P, Y = g.vector, g.scalar, g.tensor, g.sync
     rank = T.rank_of(core)
@@ -99,11 +112,14 @@ def rank_program(g, core, T, topo):
             role, own = "partner", c
         if mate[c] == core:
             role, own = "mate", c
+        if helper[c] == core:
+            role, own = "helper", c
     if role is None:
         return
     me = cores.index(own)
     is_owner = role == "rank"
-    up = role != "partner"
+    side_b = role in ("mate", "helper")
+    up = role in ("rank", "mate")
     NL = LISTS[0] if up else LISTS[1]
     NC = 16 * NL
     NS, NB = NC + 2, 4 * (NC + 2)
@@ -118,14 +134,14 @@ def rank_program(g, core, T, topo):
         return {name: buf[:, stride * k:stride * k + n] for k, name in enumerate(names)}
 
     B = {}
-    B.update(cut(T.i96, CM, NC, ["hi", "hj", "xi", "xj", "xh", "xk"]))
-    B.update(cut(T.b96, CM, NC, ["lo_a", "hi_a", "lo_b", "hi_b", "key", "keyb"]))
-    B.update(cut(T.f96, CM, NC, ["tk", "nm", "dmp", "dump0", "dumpc", "t4", "t5", "kk", "dk"]))
+    B.update(cut(T.i96, CM, NC, ["x", "xh"]))
+    B.update(cut(T.b96, CM, NC, ["lo", "hi", "key"]))
+    B.update(cut(T.f96, CM, NC, ["tk", "dmp", "dump0", "dumpc", "t5"]))
     B.update(cut(T.i16, 16, 16, ["ip", "pm", "pg", "p8"]))
     B.update(cut(T.f16, 16, 16, ["pmf", "pgf", "ir", "mask16", "p8f", "mask8", "mask64", "seg8"]))
     B.update(cut(T.i128, 128, 128, ["im", "mm"]))
     pcol, gcol = T.f16[:, 0:1], T.f16[:, 16:17]
-    li, lj = T.li[:, 0:NC], T.lj[:, 0:NC]
+    l_in = [T.lij[:, 0:NC], T.lij[:, NC:2 * NC]]
 
     def wait(q, qn, deps):
         for t in deps:
@@ -179,7 +195,7 @@ def rank_program(g, core, T, topo):
         return at(A.activation(out, in_, AF.Copy, **kw))
 
     tself = False
-    nraw = 8 * NL
+    nraw = 2 * EL * NL
     first = LISTS[0]
     if is_owner:
         ql = rank if rank < first else rank - first
@@ -188,13 +204,16 @@ def rank_program(g, core, T, topo):
         if rank < first:
             dma(Y, "y", T.rini[ql], T.pi[:], "dself")
             dma(A, "a", T.rinj[ql], T.pj[:], "dself")
-            nraw -= 8
+            nraw -= 2 * EL
             tself = True
+        t_ta0 = dma(Y, "y", T.sta[:, 0:2048], T.ta[:, 0:2048], "dta0")
     F = {"allow_small_or_imprecise_dtypes": True}
     c_ip = gt(g.iota(B["ip"], [[0, 16]], 0, 1))
     c_ir = gt(g.iota(B["ir"], [[1, 16]], 0, 0, **F))
     c_dd = gt(g.iota(T.dd[:], [[1, 148]], -1, -1, **F))
+    c_du = gt(g.iota(B["dump0"], [[16, NC]], SLOTS - 16 * CAP - (0 if up else CAP - 1), 0, **F))
     if is_owner:
+        c_im = gt(g.iota(B["im"], [[1, 128]], 0, 0))
         offc = [c for c in cores if topo.chip(c) != topo.chip(core)]
         mo = topo.mask(core, offc[0])
         mn = topo.mask(core, partner[core]) & ~mo
@@ -202,12 +221,12 @@ def rank_program(g, core, T, topo):
         def raw(parts, sem):
             tr = []
             for dl, mask in parts:
-                b = bits(mask)
+                b = bits(mask)[::2]
                 ids = []
                 for c in dl:
                     rid, pid = dst(c)
                     ids.append(DstId(rid=rid, pnc=pid))
-                for src, buf, eng in ((T.rawi, T.rini, b[:4]), (T.rawj, T.rinj, b[4:8])):
+                for src, buf, eng in ((T.rawi, T.rini, b[:EL]), (T.rawj, T.rinj, b[EL:2 * EL])):
                     tr.append(RemoteDMATransfer(dst_ids=ids, dma_engine_mask=sum(eng), remote_sem=S["rawin"],
                                                 srcs=[src[:]], dsts=[buf[ql] for _ in ids], alu_op=0))
             g.remote_dma_fused(tr, local_sem=S[sem])
@@ -216,14 +235,9 @@ def rank_program(g, core, T, topo):
         wait(g, "g", [("draw", 32)])
         raw([([c for c in to if topo.chip(c) != topo.chip(core)], mo),
              ([c for c in to if topo.chip(c) == topo.chip(core)], mn)], "rawsent")
-        if rank < first:
-            raw([([mate[c] for c in cores], mo)], "rawsent2")
-        dma(Y, "y", T.sta[:, 0:1024], T.ta[:, 0:1024], "dta0", deps=[("rawsent", 16)])
+        raw([([(mate if rank < first else helper)[c] for c in cores], mo)], "rawsent2")
 
-    c_du = gt(g.iota(B["dump0"], [[16, NC]], SLOTS, 0, **F))
-    if is_owner:
-        c_im = gt(g.iota(B["im"], [[1, 128]], 0, 0))
-    else:
+    if side_b:
         c_to = gt(g.iota(T.tof[:, 0:8 * NL], [[16, NL], [0, 8]], 0, 0, **F))
         c_bd = gt(g.iota(T.tl[:, 0:128 * NL], [[0, NL], [1, 8], [0, 16]], 0, 0, **F))
     k_pm = ts(B["pm"], B["ip"], 15, None, OP.bitwise_and, deps=[c_ip])
@@ -241,142 +255,162 @@ def rank_program(g, core, T, topo):
     k_mb = ms(T.maskb[:, 0:NB], 1.0)
     for c in range(4):
         k_mb = ms(T.maskb[:, c * NS + 2:c * NS + 3], 0.0, deps=[k_mb])
-    k_du = ts(B["dumpc"], B["dump0"], pcol, None, OP.add, deps=[c_du, k_pmf])
-
-    def late_constants():
-        k1 = ts(T.toff[:, 0:8 * NL], T.tof[:, 0:8 * NL], pcol, None, OP.add, deps=[c_to])
-        k2 = ts(T.bd[:, 0:128 * NL], T.tl[:, 0:128 * NL], gcol, None, OP.is_equal, deps=[c_bd, k_pgf])
-        z = ms(T.wb[:, 0:SLOTS], 0.0)
-        return k1, k2, z
-
+    k_du = ts(B["dumpc"], B["dump0"], pcol, 1.0 / 16, OP.add, OP.mult, deps=[c_du, k_pmf])
+    k_idf = ts(T.idf[:], T.dd[:, 1:129], 0.0, None, OP.is_equal)
+    k_id5 = ts(T.id5[:], T.dd[:, 1:129], 0.0, float(CAP), OP.is_equal, OP.mult)
+    k_idh = ts(T.idh[:], T.dd[:, 1:129], 0.0, 1.0 if up else -1.0, OP.is_equal, OP.mult)
     if is_owner:
         k_mm = ts(B["mm"], B["im"], 15, None, OP.bitwise_and, deps=[c_im])
         k_m8 = tt(B["mask8"], B["pgf"], B["ir"], OP.is_equal, deps=[k_pgf])
         k_mmf = vcopy(T.mmf[:], B["mm"], deps=[k_mm])
         k_m64 = ts(B["mask64"], B["mask8"], 64.0, None, OP.mult, deps=[k_m8])
         k_rep = ts(T.rep16[:], T.mmf[:], pcol, None, OP.is_equal, deps=[k_mmf])
-    if role == "mate":
-        k_to, k_bd, zwb = late_constants()
-    else:
-        zwa = ms(T.wa[:, 0:SLOTS], 0.0)
+    zwa = ms(T.wa[:, 0:SLOTS], 0.0)
+    if side_b:
+        k_to = ts(T.toff[:, 0:8 * NL], T.tof[:, 0:8 * NL], pcol, None, OP.add, deps=[c_to])
+        k_bd = ts(T.bd[:, 0:128 * NL], T.tl[:, 0:128 * NL], gcol, None, OP.is_equal, deps=[c_bd, k_pgf])
 
-    for q, qn, src, out, sem in ((Y, "y", T.rini, T.li, "dl"), (A, "a", T.rinj, T.lj, "dl2")):
+    for q, qn, src, out, sem in ((Y, "y", T.rini, l_in[0], "dl"), (A, "a", T.rinj, l_in[1], "dl2")):
         wait(q, qn, [("rawin", nraw), ("dself", 32) if tself else None])
-        dma(q, qn, out[0:NC, 0:NC], src[0:NL, 0:NC, :], sem)
-        for k in range(NL):
-            dma(q, qn, out[NC:128, 16 * k:16 * k + 16], src[k, NC:128, :], sem)
-    l_i, l_j = ("dl", cnt["dl"]), ("dl2", cnt["dl2"])
+        dma(q, qn, out, src[0:NL], sem)
+    l_i, l_j = ("dl", 16), ("dl2", 16)
     if is_owner:
-        for a in range(1, 8):
-            t_ta = dma(Y, "y", T.sta[:, 1024 * a:1024 * a + 1024], T.ta[:, 1024 * a:1024 * a + 1024], "dta1")
+        wait(Y, "y", [l_i, l_j])
+        for a in range(1, 4):
+            t_ta = dma(Y, "y", T.sta[:, 2048 * a:2048 * a + 2048], T.ta[:, 2048 * a:2048 * a + 2048], "dta1")
         for a in range(4):
             t_tb = dma(Y, "y", T.stb[:, 2048 * a:2048 * a + 2048], T.tb[:, 2048 * a:2048 * a + 2048], "dtb")
 
-    banks = [T.sc0, T.sc1, T.un]
-    bank_free = [None, None, None]
+    banks = [T.sc0, T.un]
+    bank_free = [None, None]
 
-    def places(l, x, xh, lo, hi):
-        ts(B[x], l, 63, None, OP.bitwise_and)
-        t = ts(B[xh], l, 6, 127, OP.logical_shift_right, OP.bitwise_and)
-        vcopy(B[lo], B[x], deps=[t])
-        return vcopy(B[hi], B[xh])
+    def places(l, dep):
+        t1 = ts(B["x"], l, 63, None, OP.bitwise_and, deps=[dep])
+        t2 = ts(B["xh"], l, 6, 127, OP.logical_shift_right, OP.bitwise_and)
+        vcopy(B["lo"], B["x"], deps=[t1])
+        return vcopy(B["hi"], B["xh"], deps=[t2])
 
-    def unwrap(lo, hi, out, blocks, dep):
-        last = None
-        for blk in blocks:
-            bk = banks[blk % 3]
-            for k in range(4):
-                r = 4 * blk + k
-                o = bk[:, NC * k:NC * k + NC]
-                mm(o, T.zz[:, 132 * r + 1:132 * r + 129], hi, True, False, deps=[dep, k_z, bank_free[blk % 3]])
-                last = mm(o, T.zz[:, 132 * r:132 * r + 128], lo, False, True)
-            for k in range(4):
-                r = 4 * blk + k
-                bank_free[blk % 3] = act(out[:, r:16 * NC:16], bk[:, NC * k:NC * k + NC], deps=[last])
-        return bank_free[blocks[-1] % 3]
+    def keys(mine):
+        t = ts(T.h96[:, 0:2 * NC], T.lij[:, 0:2 * NC], 13, None, OP.logical_shift_right, deps=[l_i, l_j])
+        h = [T.h96[:, 0:NC], T.h96[:, NC:2 * NC]]
+        t = ts(B["tk"], h[mine], float(me), 16.0, OP.not_equal, OP.mult, deps=[t])
+        return tt(B["key"], B["tk"], h[1 - mine], OP.max, deps=[t])
 
-    def one_hots(key, dep, pdep):
+    def unwrap(lo, hi, out, blk, dep):
+        bk = banks[blk % 2]
+        for k in range(4):
+            r = 4 * blk + k
+            o = bk[:, NC * k:NC * k + NC]
+            mm(o, T.zz[:, 132 * r + 1:132 * r + 129], hi, True, False, deps=[dep, k_z, bank_free[blk % 2]])
+            last = mm(o, T.zz[:, 132 * r:132 * r + 128], lo, False, True)
+        for k in range(4):
+            r = 4 * blk + k
+            t = act(out[:, r:16 * NC:16], bk[:, NC * k:NC * k + NC], deps=[last])
+        bank_free[blk % 2] = t
+        return t
+
+    def one_hots(key, dep):
         toks = []
         for c in range(NR):
             o = ts(T.oh[:, 4 + NS * c:4 + NS * c + NC], key, float(c), None, OP.is_equal, deps=[dep, k_oh])
             if c % 4 == 3:
                 x = 2 + NB * (c // 4)
                 out = T.cum[:, 512 * (c // 4):512 * (c // 4) + NB]
-                mm(out, T.tri[:], T.oh[:, x:x + NB], True, False, deps=[o, k_tri, k_trc, pdep])
+                mm(out, T.tri[:], T.oh[:, x:x + NB], True, False, deps=[o, k_tri, k_trc])
                 toks.append(mm(out, T.trc[:], T.oh[:, x - 1:x - 1 + NB], False, True))
-        nm = ts(B["nm"], key, 16.0, None, OP.is_ge)
-        kk = ts(B["kk"], key, float(CAP), 0.0 if up else float(CAP - 1), OP.mult, OP.add)
-        d = tt(B["dk"], B["dumpc"], B["kk"], OP.subtract, deps=[kk, k_du])
-        e = tt(B["dk"], B["nm"], B["dk"], OP.mult, deps=[d])
-        dm = tt(B["dmp"], B["dk"], B["kk"], OP.add, deps=[e])
-        return toks, dm
+        return toks
 
-    def slots(toks, dm, sl):
-        pq = T.pq
+    def dumps():
+        d = tt(B["dmp"], B["tk"], B["dumpc"], OP.mult, deps=[k_du])
+        mm(T.sc1[:, 0:NC], T.idf[:], B["dmp"], True, False, deps=[d, k_idf])
+        mm(T.sc1[:, 0:NC], T.id5[:], B["key"], False, False, deps=[k_id5])
+
+    def scans(toks):
         m = []
         for k in range(3):
             o = (T.ofp, T.sm, T.ofp)[k][:, 0:NB]
-            c = T.cum[:, 512 * k:512 * k + NB]
-            wait(V, "v", [toks[k], k_mb, ("v", cnt["v"])])
-            s = vt(V.tensor_tensor_scan(o, T.maskb[:, 0:NB], c, 0.0, OP.mult, OP.add))
-            m.append(tt(pq[:, 0:NB] if k == 1 else c, o, T.oh[:, 2 + NB * k:2 + NB * k + NB], OP.mult, deps=[s]))
-        a1 = tt(pq[:, 512:512 + NB], T.cum[:, 0:NB], pq[:, 0:NB], OP.add, deps=[m[1]])
-        a2 = tt(pq[:, 1024:1024 + NB], T.cum[:, 1024:1024 + NB], pq[:, 512:512 + NB], OP.add, deps=[a1, m[2]])
-        a3 = tt(pq[:, 0:2 * NS], pq[:, 1024:1024 + 2 * NS], pq[:, 1024 + 2 * NS:1024 + NB], OP.add, deps=[a2])
-        a4 = tt(B["t4"], pq[:, 2:NS], pq[:, NS + 2:2 * NS], OP.add, deps=[a3])
-        a5 = tt(B["t5"], B["dmp"], B["t4"], OP.add if up else OP.subtract, deps=[a4, dm])
-        return vcopy(sl[:, 0:NC], B["t5"], deps=[a5])
+            wait(V, "v", [toks[k], k_mb])
+            s = vt(V.tensor_tensor_scan(o, T.maskb[:, 0:NB], T.cum[:, 512 * k:512 * k + NB], 0.0, OP.mult, OP.add))
+            m.append(tt(T.xq[:, NB * k:NB * k + NB], o, T.oh[:, 2 + NB * k:2 + NB * k + NB], OP.mult, deps=[s]))
+        return m
+
+    def sums(k, m):
+        for c in range(4 * k, 4 * k + 4):
+            p = mm(T.sc1[:, 0:NC], T.idh[:], T.xq[:, NS * c + 2:NS * c + 2 + NC], False, c == NR - 1, deps=[m, k_idh])
+        return p
+
+    def slots(p, sl):
+        if up:
+            return vcopy(sl[:, 0:NC], T.sc1[:, 0:NC], deps=[p])
+        return ts(sl[:, 0:NC], T.sc1[:, 0:NC], float(CAP - 1), None, OP.add, deps=[p])
 
     def scatter(win, sl, vals, deps):
         wait(V, "v", deps)
         return vt(V.tensor_copy(win[:, 0:SLOTS + 16 * NC].indirect(sl[:, 0:NC]), vals[:, 0:16 * NC]))
 
-    def wrap1(win, dep):
-        for ch in range(48):
-            t = mm(T.sm[:, 2 * ch:2 * ch + 2], win[:, 128 * ch:128 * ch + 128], T.sel[:, 0:2], deps=[dep, k_sel])
+    def wrap1(win, dep, classes, out):
+        for i, ch in enumerate([4 * c + q for c in classes for q in range(4)]):
+            t = mm(out[:, 2 * i:2 * i + 2], win[:, 128 * ch:128 * ch + 128], T.sel[:, 0:2], deps=[dep, k_sel])
         return t
 
-    def wrap2(x, dep):
+    def wrap2(x, n, out, dep):
         for b in range(8):
-            o = T.ofp[:, b:384:8]
-            mm(o, T.lb[:, 256 * b:256 * b + 128], x[:, 0:96:2], True, False, deps=[dep, k_lb])
-            t = mm(o, T.lb[:, 256 * b + 128:256 * b + 256], x[:, 1:96:2], False, True)
+            o = out[:, b:32 * n:8]
+            mm(o, T.lb[:, 256 * b:256 * b + 128], x[:, 0:8 * n:2], True, False, deps=[dep, k_lb])
+            t = mm(o, T.lb[:, 256 * b + 128:256 * b + 256], x[:, 1:8 * n:2], False, True)
         return t
 
     def turn(dep):
-        f5 = T.f96[:, 6 * CM:6 * CM + NC]
-        wait(V, "v", [dep, k_to, k_bd])
-        t = vt(V.tensor_copy(T.tl[:, 0:128 * NL], f5.indirect(T.toff[:, 0:8 * NL])))
+        t = ts(B["t5"], T.sc1[:, 0:NC], 0.0 if up else float(CAP - 1), None, OP.add, deps=[dep])
+        wait(V, "v", [t, k_to, k_bd])
+        t = vt(V.tensor_copy(T.tl[:, 0:128 * NL], B["t5"].indirect(T.toff[:, 0:8 * NL])))
         t = tt(T.tl[:, 0:128 * NL], T.tl[:, 0:128 * NL], T.bd[:, 0:128 * NL], OP.mult, deps=[t])
         for c in range(NL):
-            mm(T.un[:, c:NC:NL], T.tl[:, 128 * c:128 * c + 128], B["mask16"], deps=[t, u_b])
-            p = mm(T.un[:, 128 + 16 * c:144 + 16 * c], T.tl[:, 128 * c:128 * c + 128], B["mask16"])
-        t = vcopy(T.slt[:, 0:NC], T.un[:, 128:128 + NC], deps=[p])
-        return vcopy(T.slt[0:NC, 0:NC], T.un[0:NC, 0:NC], deps=[t])
+            p = mm(T.un[:, c:NC:NL], T.tl[:, 128 * c:128 * c + 128], B["mask16"], deps=[t, u])
+        return vcopy(T.slt[:, 0:NC], T.un[:, 0:NC], deps=[p])
 
     def send(out, src, name, dep):
         rid, pid = dst(own)
-        mask = topo.mask(core, own)
+        mask = sum(bits(topo.mask(core, own))[:NE])
         wait(g, "g", [dep])
         g.remote_dma(out_ap=out, in_ap=src, remote_sem=S[name], local_sem=S["xsent"], pid=pid, routing_id=rid,
                      dma_engine_mask=mask)
-        return len(bits(mask))
+        return NE
 
-    if role == "mate":
-        b_hj = ts(B["hj"], lj, 13, None, OP.logical_shift_right, deps=[l_j])
-        b_hb = places(lj, "xj", "xk", "lo_b", "hi_b")
-        ts(B["tk"], B["hj"], float(me), 16.0, OP.not_equal, OP.mult)
-        b_hi = ts(B["hi"], li, 13, None, OP.logical_shift_right, deps=[l_i])
-        k_kb = tt(B["keyb"], B["tk"], B["hi"], OP.add, deps=[b_hi])
-        unwrap(B["lo_b"], B["hi_b"], T.vb, [0, 1], b_hb)
-        toks, dm = one_hots(B["keyb"], k_kb, None)
-        u_b = unwrap(B["lo_b"], B["hi_b"], T.vb, [2, 3], b_hb)
-        sl_b = slots(toks, dm, T.slb)
-        sc_b = scatter(T.wb, T.slb, T.vb, [sl_b, u_b, zwb])
-        w_b = wrap1(T.wb, sc_b)
-        x_b = vcopy(T.xb[:], T.sm[:, 0:96], deps=[w_b])
-        n = send(T.xmb[:], T.xb[:], "xmb", x_b)
-        n += send(T.slt[:], T.slt[:], "slm", turn(sl_b))
+    def arrival(h):
+        if h == me:
+            return 0.0
+        i = order[h].index(me)
+        if topo.chip(cores[h]) == topo.chip(own):
+            return 3.0 + 0.1 * i
+        return (2.0 if i < 3 else 0.0) + 1.2 * i + (2.0 if (cores[h], own) in relay else 0.0)
+
+    row = sorted(range(NR), key=lambda h: (arrival(h), h))
+
+    mine = 1 if side_b else 0
+    k_key = keys(mine)
+    toks = one_hots(B["key"], k_key)
+    dumps()
+    k_pl = places(l_in[mine], (l_i, l_j)[mine])
+    m = scans(toks)
+    for blk in range(4):
+        u = unwrap(B["lo"], B["hi"], T.va, blk, k_pl)
+        if blk < 3:
+            p = sums(blk, m[blk])
+    sl = slots(p, T.sla)
+    sc = scatter(T.wa, T.sla, T.va, [sl, u, zwa])
+    n = 0
+    X1, X2 = (0, 8 * PA), (8 * PA, 96)
+    seq = row if side_b else order[me]
+    w1 = wrap1(T.wa, sc, seq[:PA], T.sm)
+    w2 = wrap1(T.wa, sc, seq[PA:], T.cum)
+    if not is_owner:
+        nx = {"partner": "xpa", "mate": "xmb", "helper": "xpb"}[role]
+        for (a, e), ps, wt, sfx in ((X1, T.sm, w1, ""), (X2, T.cum, w2, "2")):
+            x = vcopy(T.xa[:, a:e], ps[:, 0:e - a], deps=[wt])
+            n += send(T[nx][:, a:e], T.xa[:, a:e], nx + sfx, x)
+        if side_b:
+            n += send((T.slt if up else T.slp)[:, 0:NC], T.slt[:, 0:NC], "slm" if up else "slp", turn(x))
         jobs = [(s, d) for (s, d), r in relay.items() if r == core]
         for s, d in sorted(jobs, key=lambda sd: order[cores.index(sd[0])].index(cores.index(sd[1]))):
             h, k = cores.index(s), slot_at_relay(cores, topo, d)
@@ -389,39 +423,6 @@ def rank_program(g, core, T, topo):
         wait(g, "g", [(k, cnt[k]) for k in ("v", "a", "p", "gp")])
         return
 
-    b_hi = ts(B["hi"], li, 13, None, OP.logical_shift_right, deps=[l_i])
-    b_ha = places(li, "xi", "xh", "lo_a", "hi_a")
-    ts(B["tk"], B["hi"], float(me), 16.0, OP.not_equal, OP.mult)
-    b_hj = ts(B["hj"], lj, 13, None, OP.logical_shift_right, deps=[l_j])
-    k_key = tt(B["key"], B["tk"], B["hj"], OP.add, deps=[b_hj])
-    unwrap(B["lo_a"], B["hi_a"], T.va, [0, 1], b_ha)
-    toks, dm = one_hots(B["key"], k_key, None)
-    u_a = unwrap(B["lo_a"], B["hi_a"], T.va, [2, 3], b_ha)
-    sl_a = slots(toks, dm, T.sla)
-
-    if role == "partner":
-        b_hb = places(lj, "xj", "xk", "lo_b", "hi_b")
-        u_b = unwrap(B["lo_b"], B["hi_b"], T.vb, [0, 1, 2, 3], b_hb)
-        sc_a = scatter(T.wa, T.sla, T.va, [sl_a, u_a, zwa])
-        w_a = wrap1(T.wa, sc_a)
-        b_t = ts(B["tk"], B["hj"], float(me), 16.0, OP.not_equal, OP.mult)
-        k_kb = tt(B["keyb"], B["tk"], B["hi"], OP.add, deps=[b_t])
-        toks, dm = one_hots(B["keyb"], k_kb, sl_a)
-        x_a = vcopy(T.xa[:], T.sm[:, 0:96], deps=[w_a])
-        n = send(T.xpa[:], T.xa[:], "xpa", x_a)
-        k_to, k_bd, zwb = late_constants()
-        sl_b = slots(toks, dm, T.slb)
-        sc_b = scatter(T.wb, T.slb, T.vb, [sl_b, u_b, zwb])
-        w_b = wrap1(T.wb, sc_b)
-        x_b = vcopy(T.xb[:], T.sm[:, 0:96], deps=[w_b])
-        n += send(T.xpb[:], T.xb[:], "xpb", x_b)
-        n += send(T.slp[:], T.slt[:, 0:NC], "slp", turn(sl_b))
-        wait(g, "g", [("xsent", n)])
-        wait(g, "g", [(k, cnt[k]) for k in ("v", "a", "p", "gp")])
-        return
-
-    sc_a = scatter(T.wa, T.sla, T.va, [sl_a, u_a, zwa])
-    w_a = wrap1(T.wa, sc_a)
     for b in range(8):
         for w in range(2):
             c = (80 if w else 96) + b
@@ -432,79 +433,89 @@ def rank_program(g, core, T, topo):
     zsw = ms(T.sw[:, SLOTS:WIN], 0.0)
     k_p8f = vcopy(B["p8f"], B["p8"], deps=[k_p8])
     k_seg = tt(B["seg8"], B["p8f"], B["ir"], OP.is_equal, deps=[k_p8f])
-    np = len(bits(topo.mask(partner[core], core)))
-    nm_ = len(bits(topo.mask(mate[core], core)))
-    x_a = tt(T.xa[:], T.sm[:, 0:96], T.xpa[:], OP.add, deps=[w_a, ("xpa", np)])
-    p_a = wrap2(T.xa, x_a)
-    o_a = vcopy(T.offa[:], T.ofp[:, 0:384], deps=[p_a])
 
+    def offsets_a(a, e, ps, wt, name, out):
+        x = tt(T.xa[:, a:e], ps[:, 0:e - a], T.xpa[:, a:e], OP.add, deps=[wt, (name, NE)])
+        return wrap2(T.xa[:, a:e], (e - a) // 8, out, x)
+
+    def offsets_a2(a, e, out, p):
+        return vcopy(T.offa[:, 4 * a:4 * e], out[:, 0:4 * (e - a)], deps=[p])
+
+    o_a = offsets_a2(*X1, T.ofp, offsets_a(*X1, T.sm, w1, "xpa", T.ofp))
+    out2 = T.cum[:, 512:1024]
     full = {}
     nsentp = 0
-    for b in order[me]:
+    sent = []
+    noff = 0
+    for i, b in enumerate(order[me]):
         d = cores[b]
-        src = T.sta[:, 0:RC].indirect(T.offa[:, 32 * b:32 * b + 32])
+        off = topo.chip(d) != topo.chip(core)
+        noff += off
+        on_a = b == me or (off and noff in (1, 3, 4, 5, 7))
+        src = T.sta[:, 0:RC].indirect(T.offa[:, 32 * i:32 * i + 32])
         blk = T.sb[:, CAP * b:CAP * b + CAP]
-        deps = [o_a, ("dta0", 16), t_ta]
-        if topo.chip(d) == topo.chip(core):
-            tg = vcopy(blk, src, deps=deps)
-        else:
-            tg = act(blk, src, deps=deps)
-        full[b] = tg
+        if i == PA:
+            o_a = offsets_a2(*X2, out2, p2)
+        deps = [o_a, t_ta0, t_ta]
+        full[b] = act(blk, src, deps=deps) if on_a else vcopy(blk, src, deps=deps)
+        if i == 1:
+            p2 = offsets_a(*X2, T.cum, w2, "xpa2", out2)
         if b == me:
             continue
-        wait(g, "g", [tg])
+        wait(g, "g", [full[b]])
+        out, sem, to = T.rb[:, CAP * me:CAP * me + CAP], "pay%d" % me, d
         if (core, d) in relay:
-            to = relay[core, d]
-            k = slot_at_relay(cores, topo, d)
+            k, to = slot_at_relay(cores, topo, d), relay[core, d]
             out, sem = T.rb[:, CAP * k:CAP * k + CAP], "rl%d" % k
-        else:
-            to = d
-            out, sem = T.rb[:, CAP * me:CAP * me + CAP], "pay%d" % me
         mask = topo.mask(core, to)
-        if topo.chip(to) == topo.chip(core):
+        lsem = "psent"
+        if off:
+            if noff > WINDOW:
+                wait(g, "g", [sent[noff - 1 - WINDOW]])
+            lsem = "ps%d" % (noff - 1)
+            sent.append((lsem, 8))
+        else:
             mask &= ~mo
+            nsentp += 8
         rid, pid = dst(to)
-        g.remote_dma(out_ap=out, in_ap=blk, remote_sem=S[sem], local_sem=S["psent"], pid=pid, routing_id=rid,
+        g.remote_dma(out_ap=out, in_ap=blk, remote_sem=S[sem], local_sem=S[lsem], pid=pid, routing_id=rid,
                      dma_engine_mask=mask)
-        nsentp += 8
 
-    x_b = tt(T.xb[:], T.xpb[:], T.xmb[:], OP.add, deps=[("xpb", np), ("xmb", nm_)])
-    p_b = wrap2(T.xb, x_b)
-    o_b = vcopy(T.offb[:], T.ofp[:, 0:384], deps=[p_b])
+    def offsets_b(a, e, sfx):
+        x = tt(T.xb[:, a:e], T.xpb[:, a:e], T.xmb[:, a:e], OP.add, deps=[("xpb" + sfx, NE), ("xmb" + sfx, NE)])
+        return wrap2(T.xb[:, a:e], (e - a) // 8, T.ofp[:, 4 * a:4 * e], x)
 
-    def arrival(h):
-        if h == me:
-            return 2.0
-        same = topo.chip(cores[h]) == topo.chip(core)
-        row = [b for b in order[h] if (topo.chip(cores[b]) == topo.chip(cores[h])) == same]
-        return row.index(me) + 1.0 + (2.5 if (cores[h], core) in relay else 0.0)
+    def offsets_b2(a, e, p):
+        return vcopy(T.offb[:, 4 * a:4 * e], T.ofp[:, 4 * a:4 * e], deps=[p])
 
+    o_b = offsets_b2(*X1, offsets_b(*X1, ""))
     scs = [T.sc0[:], T.sc1[:], T.un[:]] + [T.cum[:, 512 * k:512 * k + 512] for k in range(3)]
     pm_ = [None, None]
-    pc_ = [u_a, u_a, u_a, sl_a, sl_a, sl_a]
-    for n, h in enumerate(sorted(range(NR), key=lambda h: (arrival(h), h))):
-        k, j = n % 2, n % 6
-        pr = T.prod[:, CAP * k:CAP * k + CAP]
-        blk = T.rb
-        if h == me:
-            blk = T.sb
-        wait(V, "v", [o_b, t_tb, full[me] if h == me else ("pay%d" % h, 8), pm_[k]])
-        t = vt(V.tensor_tensor(pr, T.stb[:, 0:RC].indirect(T.offb[:, 32 * h:32 * h + 32]),
-                               blk[:, CAP * h:CAP * h + CAP], OP.mult))
-        pm_[k] = mm(scs[j], T.onesf[:], pr, deps=[t, k_of, pc_[j]])
-        pc_[j] = act(T.sw[:, CAP * h:CAP * h + CAP], scs[j], deps=[pm_[k]])
+    pc_ = [u, sl, u, sl, sl, sl]
+    n = 0
+    for nh, h in enumerate(row):
+        blk = T.sb if h == me else T.rb
+        ready = full[me] if h == me else ("pay%d" % h, 8)
+        for a, e in ([(0, CAP // 2), (CAP // 2, CAP)] if h == row[-1] else [(0, CAP)]):
+            k, j = n % 2, n % 6
+            n += 1
+            pr = T.prod[:, CAP * k:CAP * k + e - a]
+            wait(V, "v", [o_b, t_tb, ready, pm_[k]])
+            t = vt(V.tensor_tensor(pr, T.stb[:, 0:RC].indirect(T.offb[:, 32 * nh + a // 16:32 * nh + e // 16]),
+                                   blk[:, CAP * h + a:CAP * h + e], OP.mult))
+            pm_[k] = mm(scs[j][:, 0:e - a], T.onesf[:], pr, deps=[t, k_of, pc_[j]])
+            if nh == 0:
+                p_b2 = offsets_b(*X2, "2")
+            if nh == 2:
+                o_b = offsets_b2(*X2, p_b2)
+            pc_[j] = act(T.sw[:, CAP * h + a:CAP * h + e], scs[j][:, 0:e - a], deps=[pm_[k]])
 
-    wait(V, "v", pc_ + [zsw, ("slm", nm_)])
-    f0 = vt(V.tensor_copy(T.r0[:], T.sw[:, 0:WIN].indirect(T.slt[:, 0:NC])))
-    wait(A, "a", pc_ + [zsw, ("slp", np)])
-    f1 = at(A.activation(T.r1[:], T.sw[:, 0:WIN].indirect(T.slp[:]), AF.Copy))
-    d0 = 0
-    for q, qn, R, f, sem, n in ((Y, "y", T.r0, f0, "dd0", LISTS[0]), (A, "a", T.r1, f1, "dd1", LISTS[1])):
-        wait(q, qn, [f])
-        dma(q, qn, T.dres[d0:d0 + n, 0:16 * n, :], R[0:16 * n:16, :], sem)
-        for p in range(16 * n, 128, 16):
-            dma(q, qn, T.dres[d0:d0 + n, p:p + 16, :], R[p:p + 1, :], sem)
-        d0 += n
+    wait(V, "v", pc_ + [zsw, ("slm", NE)])
+    f0 = vt(V.tensor_copy(T.r0[:], T.sw[:, 0:WIN].indirect(T.slt[:, 0:16 * LISTS[0]])))
+    wait(A, "a", pc_ + [zsw, ("slp", NE)])
+    f1 = at(A.activation(T.r1[:], T.sw[:, 0:WIN].indirect(T.slp[:, 0:16 * LISTS[1]]), AF.Copy))
+    dma(Y, "y", T.dres[0:first], T.r0[0:128:16, :], "dd0", deps=[f0])
+    dma(A, "a", T.dres[first:NR], T.r1[0:128:16, :], "dd1", deps=[f1])
     td = [("dd0", cnt["dd0"]), ("dd1", cnt["dd1"])]
     wait(g, "g", td)
     offr = [b for b in range(NR) if topo.chip(cores[b]) != topo.chip(core)]
@@ -524,8 +535,7 @@ def rank_program(g, core, T, topo):
     py = mm(T.ofp[0:8, 0:256], T.f16[0:96, 112:120], T.res[:], deps=[t_x, k_seg])
     ty = vcopy(T.ys[:], T.ofp[0:8, 0:256], deps=[py])
     dma(Y, "y", T.y[:], T.ys[:], "dy", deps=[ty])
-    wait(g, "g", [("dy", 16), ("rawsent", 16), ("psent", nsentp), ("ressent", nres), ("dta0", 16),
-                  ("rawsent2", 8) if rank < first else None])
+    wait(g, "g", [("dy", 16), ("rawsent", 4 * EL), ("rawsent2", 2 * EL), ("psent", nsentp), ("ressent", nres), t_ta0] + sent)
     wait(g, "g", [(k, cnt[k]) for k in ("v", "a", "p", "gp")])
 
 

from concourse.bass import DstId, RemoteDMATransfer
from concourse.mybir import AluOpType as OP, ActivationFunctionType as AF

NR, RC, CAP = 12, 8192, 512
LISTS = (7, 5)
CM = 16 * max(LISTS)
SLOTS = NR * CAP
WIN = SLOTS + 16 * CM
OHW = 2 + NR * (CM + 2)
PA = 4
WINDOW = 3
NE = 4
EL = 2

SCRATCH = {
    "rawi": ("dram", [128, 16], "int32"), "rawj": ("dram", [128, 16], "int32"),
    "rini": ("dram", [CM // 16, 128, 16], "int32"), "rinj": ("dram", [CM // 16, 128, 16], "int32"),
    "dres": ("dram", [NR, 128, 16], "float32"), "resd": ("dram", [NR, 128, 16], "float32"),
    "sta": ("sbuf", [128, RC], "float32"), "stb": ("sbuf", [128, RC], "float32"),
    "sb": ("sbuf", [128, SLOTS], "float32"), "rb": ("sbuf", [128, SLOTS], "float32"),
    "wa": ("sbuf", [128, WIN], "bfloat16"),
    "sw": ("sbuf", [128, WIN], "float32"),
    "r0": ("sbuf", [128, 256 * LISTS[0]], "float32"), "r1": ("sbuf", [128, 256 * LISTS[1]], "float32"),
    "va": ("sbuf", [128, 16 * CM], "bfloat16"),
    "oh": ("sbuf", [128, OHW], "bfloat16"), "maskb": ("sbuf", [128, 4 * (CM + 2)], "bfloat16"),
    "xq": ("sbuf", [128, 12 * (CM + 2)], "float16"),
    "prod": ("sbuf", [128, 2 * CAP], "float32"),
    "lb": ("sbuf", [128, 16 * 128], "bfloat16"), "zz": ("sbuf", [128, 16 * 132], "bfloat16"),
    "lij": ("sbuf", [128, 2 * CM], "int32"), "h96": ("sbuf", [128, 2 * CM], "int32"),
    "i96": ("sbuf", [128, 2 * CM], "int32"), "b96": ("sbuf", [128, 3 * CM], "bfloat16"), "f96": ("sbuf", [128, 5 * CM], "float32"),
    "sla": ("sbuf", [128, CM], "uint16"),
    "slt": ("sbuf", [128, CM], "uint16"), "slp": ("sbuf", [128, CM], "uint16"),
    "toff": ("sbuf", [128, CM // 2], "uint16"), "tof": ("sbuf", [128, CM // 2], "float32"),
    "tl": ("sbuf", [128, 8 * CM], "float32"), "bd": ("sbuf", [128, 8 * CM], "bfloat16"),
    "xa": ("sbuf", [128, 96], "bfloat16"), "xb": ("sbuf", [128, 96], "bfloat16"),
    "xpa": ("sbuf", [128, 96], "bfloat16"), "xpb": ("sbuf", [128, 96], "bfloat16"), "xmb": ("sbuf", [128, 96], "bfloat16"),
    "offa": ("sbuf", [128, 384], "uint16"), "offb": ("sbuf", [128, 384], "uint16"),
    "i16": ("sbuf", [128, 64], "int32"), "f16": ("sbuf", [128, 128], "float32"), "sel": ("sbuf", [128, 16], "bfloat16"),
    "i128": ("sbuf", [128, 256], "int32"), "mmf": ("sbuf", [128, 128], "float32"),
    "rep16": ("sbuf", [128, 128], "bfloat16"), "dd": ("sbuf", [128, 148], "float32"), "idz": ("sbuf", [128, 148], "bfloat16"),
    "idf": ("sbuf", [128, 128], "float32"), "idh": ("sbuf", [128, 128], "float16"), "id5": ("sbuf", [128, 128], "bfloat16"),
    "tri": ("sbuf", [128, 128], "bfloat16"), "trc": ("sbuf", [128, 128], "bfloat16"), "onesf": ("sbuf", [128, 128], "float32"),
    "res": ("sbuf", [96, 256], "float32"), "ys": ("sbuf", [8, 256], "float32"),
    "cum": ("psum", [128, 1536], "float32"), "sc0": ("psum", [128, 512], "float32"), "sc1": ("psum", [128, 512], "float32"),
    "un": ("psum", [128, 512], "float32"), "sm": ("psum", [128, 512], "float32"), "ofp": ("psum", [128, 512], "float32"),
}
SEMAPHORES = (["v", "a", "p", "gp", "draw", "dself", "dl", "dl2", "dta0", "dta1", "dtb", "dd0", "dd1", "dd2", "dx", "dy",
               "rawin", "rawsent", "rawsent2", "xpa", "xpa2", "xpb", "xmb", "xpb2", "xmb2", "slp", "slm", "xsent", "psent",
               "ressent", "resin", "rlsent"] + ["pay%d" % k for k in range(NR)] + ["ps%d" % k for k in range(8)]
              + ["rl%d" % k for k in range(4)])


def bits(mask):
    return [1 << b for b in range(mask.bit_length()) if mask >> b & 1]


def plan(cores, topo):
    n = len(cores)
    chips = sorted({topo.chip(c) for c in cores})
    ncore = 8 * 16
    partner = {}
    taken = set(cores)
    for c in cores:
        p = [d for d in range(ncore) if topo.chip(d) == topo.chip(c) and topo.die(d) == topo.die(c) and d not in taken][0]
        taken.add(p)
        partner[c] = p

    def peer_index(s):
        return [c for c in cores if topo.chip(c) == topo.chip(s) and topo.die(c) == topo.die(s)].index(s)

    def mate_core(s, chip):
        cand = [r for r in range(ncore) if topo.mates(topo.chip(r), chip) and topo.die(r) == topo.die(s)
                and all(topo.may_write(r, e) for e in cores if topo.chip(e) == chip)]
        return cand[peer_index(s) % len(cand)]

    mate = {c: mate_core(c, topo.chip(c)) for c in cores}
    helper = {}
    for c in cores:
        free = [d for d in range(ncore) if topo.same_plane(topo.chip(d), topo.chip(c)) and topo.die(d) == topo.die(c)
                and topo.chip(d) not in chips and not any(topo.mates(topo.chip(d), x) for x in chips) and d not in taken]
        p = min(free, key=lambda d: (sum(topo.chip(t) == topo.chip(d) for t in helper.values()), d))
        taken.add(p)
        helper[c] = p
    x, y = [(a, b) for a in chips for b in chips if a < b and topo.same_plane(a, b)][0]
    z = [c for c in chips if c not in (x, y)][0]
    relayed = {(y, x), (y, z), (z, y)}
    relay = {(s, d): mate_core(s, topo.chip(d)) for s in cores for d in cores if (topo.chip(s), topo.chip(d)) in relayed}
    order = []
    for h in range(n):
        s = cores[h]
        far = [[b for b in range(n) if topo.chip(cores[b]) == ch] for ch in chips if ch != topo.chip(s)]
        far.sort(key=lambda L: (s, cores[L[0]]) not in relay)
        near = [b for b in range(n) if b != h and topo.chip(cores[b]) == topo.chip(s)]
        far = [L[h % 4:] + L[:h % 4] for L in far]
        near = near[h % 3:] + near[:h % 3]
        f = [b for pair in zip(far[0], far[1]) for b in pair]
        order.append(f[:3] + near + f[3:4] + [h] + f[4:])
    return partner, mate, helper, relay, order


def rank_program(g, core, T, topo):
    cores = list(T.cores)
    partner, mate, helper, relay, order = plan(cores, topo)
    S = T.sem
    V, A, P, Y = g.vector, g.scalar, g.tensor, g.sync
    rank = T.rank_of(core)
    role, own = None, core
    if rank is not None:
        role = "rank"
    for c in cores:
        if partner[c] == core:
            role, own = "partner", c
        if mate[c] == core:
            role, own = "mate", c
        if helper[c] == core:
            role, own = "helper", c
    if role is None:
        return
    me = cores.index(own)
    is_owner = role == "rank"
    side_b = role in ("mate", "helper")
    up = role in ("rank", "mate")
    NL = LISTS[0] if up else LISTS[1]
    NC = 16 * NL
    NS, NB = NC + 2, 4 * (NC + 2)
    cnt = {}
    seen = {}

    def dst(c):
        rid, pid, _ = topo.addr(c)
        return rid, pid

    def cut(buf, stride, n, names):
        return {name: buf[:, stride * k:stride * k + n] for k, name in enumerate(names)}

    B = {}
    B.update(cut(T.i96, CM, NC, ["x", "xh"]))
    B.update(cut(T.b96, CM, NC, ["lo", "hi", "key"]))
    B.update(cut(T.f96, CM, NC, ["tk", "dmp", "dump0", "dumpc", "t5"]))
    B.update(cut(T.i16, 16, 16, ["ip", "pm", "pg", "p8"]))
    B.update(cut(T.f16, 16, 16, ["pmf", "pgf", "ir", "mask16", "p8f", "mask8", "mask64", "seg8"]))
    B.update(cut(T.i128, 128, 128, ["im", "mm"]))
    pcol, gcol = T.f16[:, 0:1], T.f16[:, 16:17]
    l_in = [T.lij[:, 0:NC], T.lij[:, NC:2 * NC]]

    def wait(q, qn, deps):
        for t in deps:
            if t is None:
                continue
            name, n = t
            if seen.get((qn, name), 0) >= n:
                continue
            seen[qn, name] = n
            q.wait_ge(S[name], n)

    def mk(qn):
        def tok(inst):
            cnt[qn] = cnt.get(qn, 0) + 1
            inst.then_inc(S[qn], 1)
            return (qn, cnt[qn])
        return tok

    vt, at, pt, gt = mk("v"), mk("a"), mk("p"), mk("gp")

    def dma(q, qn, out, in_, sem, deps=()):
        wait(q, qn, deps)
        q.dma_start(out, in_).then_inc(S[sem], 16)
        cnt[sem] = cnt.get(sem, 0) + 16
        return (sem, cnt[sem])

    def ts(out, in0, s1, s2, op0, op1=None, deps=()):
        wait(V, "v", deps)
        if op1 is None:
            return vt(V.tensor_scalar(out, in0, s1, None, op0))
        return vt(V.tensor_scalar(out, in0, s1, s2, op0, op1))

    def tt(out, in0, in1, op, deps=()):
        wait(V, "v", deps)
        return vt(V.tensor_tensor(out, in0, in1, op))

    def vcopy(out, in_, deps=()):
        wait(V, "v", deps)
        return vt(V.tensor_copy(out, in_))

    def ms(ap, c, deps=()):
        wait(V, "v", deps)
        return vt(V.memset(ap, c))

    def mm(out, lhsT, rhs, start=True, stop=True, deps=()):
        wait(P, "p", deps)
        return pt(P.matmul(out, lhsT, rhs, start, stop))

    def act(out, in_, deps=(), **kw):
        wait(A, "a", deps)
        return at(A.activation(out, in_, AF.Copy, **kw))

    tself = False
    nraw = 2 * EL * NL
    first = LISTS[0]
    if is_owner:
        ql = rank if rank < first else rank - first
        dma(Y, "y", T.rawi[:], T.pi[:], "draw")
        dma(A, "a", T.rawj[:], T.pj[:], "draw")
        if rank < first:
            dma(Y, "y", T.rini[ql], T.pi[:], "dself")
            dma(A, "a", T.rinj[ql], T.pj[:], "dself")
            nraw -= 2 * EL
            tself = True
        t_ta0 = dma(Y, "y", T.sta[:, 0:2048], T.ta[:, 0:2048], "dta0")
    F = {"allow_small_or_imprecise_dtypes": True}
    c_ip = gt(g.iota(B["ip"], [[0, 16]], 0, 1))
    c_ir = gt(g.iota(B["ir"], [[1, 16]], 0, 0, **F))
    c_dd = gt(g.iota(T.dd[:], [[1, 148]], -1, -1, **F))
    c_du = gt(g.iota(B["dump0"], [[16, NC]], SLOTS - 16 * CAP - (0 if up else CAP - 1), 0, **F))
    if is_owner:
        c_im = gt(g.iota(B["im"], [[1, 128]], 0, 0))
        offc = [c for c in cores if topo.chip(c) != topo.chip(core)]
        mo = topo.mask(core, offc[0])
        mn = topo.mask(core, partner[core]) & ~mo

        def raw(parts, sem):
            tr = []
            for dl, mask in parts:
                b = bits(mask)[::2]
                ids = []
                for c in dl:
                    rid, pid = dst(c)
                    ids.append(DstId(rid=rid, pnc=pid))
                for src, buf, eng in ((T.rawi, T.rini, b[:EL]), (T.rawj, T.rinj, b[EL:2 * EL])):
                    tr.append(RemoteDMATransfer(dst_ids=ids, dma_engine_mask=sum(eng), remote_sem=S["rawin"],
                                                srcs=[src[:]], dsts=[buf[ql] for _ in ids], alu_op=0))
            g.remote_dma_fused(tr, local_sem=S[sem])

        to = [c for c in (cores if rank < first else [partner[c] for c in cores]) if c != core]
        wait(g, "g", [("draw", 32)])
        raw([([c for c in to if topo.chip(c) != topo.chip(core)], mo),
             ([c for c in to if topo.chip(c) == topo.chip(core)], mn)], "rawsent")
        raw([([(mate if rank < first else helper)[c] for c in cores], mo)], "rawsent2")

    if side_b:
        c_to = gt(g.iota(T.tof[:, 0:8 * NL], [[16, NL], [0, 8]], 0, 0, **F))
        c_bd = gt(g.iota(T.tl[:, 0:128 * NL], [[0, NL], [1, 8], [0, 16]], 0, 0, **F))
    k_pm = ts(B["pm"], B["ip"], 15, None, OP.bitwise_and, deps=[c_ip])
    k_pg = ts(B["pg"], B["ip"], 4, None, OP.arith_shift_right)
    k_pmf = vcopy(B["pmf"], B["pm"], deps=[k_pm])
    k_pgf = vcopy(B["pgf"], B["pg"], deps=[k_pg])
    k_m16 = tt(B["mask16"], B["pmf"], B["ir"], OP.is_equal, deps=[k_pmf, c_ir])
    k_id = ts(T.idz[:], T.dd[:], 0.0, None, OP.is_equal, deps=[c_dd])
    k_sel = tt(T.sel[:], B["pmf"], B["ir"], OP.is_equal)
    for r in range(16):
        k_z = act(T.zz[:, 132 * r:132 * r + 130], T.idz[:, r:r + 130], deps=[k_m16, k_id], scale=T.f16[:, 48 + r:49 + r])
    k_tri = ts(T.tri[:], T.dd[:, 1:129], 0.0, None, OP.is_gt)
    k_trc = ts(T.trc[:], T.dd[:, 1:129], 0.0, None, OP.is_le)
    k_oh = ms(T.oh[:], 0.0)
    k_mb = ms(T.maskb[:, 0:NB], 1.0)
    for c in range(4):
        k_mb = ms(T.maskb[:, c * NS + 2:c * NS + 3], 0.0, deps=[k_mb])
    k_du = ts(B["dumpc"], B["dump0"], pcol, 1.0 / 16, OP.add, OP.mult, deps=[c_du, k_pmf])
    k_idf = ts(T.idf[:], T.dd[:, 1:129], 0.0, None, OP.is_equal)
    k_id5 = ts(T.id5[:], T.dd[:, 1:129], 0.0, float(CAP), OP.is_equal, OP.mult)
    k_idh = ts(T.idh[:], T.dd[:, 1:129], 0.0, 1.0 if up else -1.0, OP.is_equal, OP.mult)
    if is_owner:
        k_mm = ts(B["mm"], B["im"], 15, None, OP.bitwise_and, deps=[c_im])
        k_m8 = tt(B["mask8"], B["pgf"], B["ir"], OP.is_equal, deps=[k_pgf])
        k_mmf = vcopy(T.mmf[:], B["mm"], deps=[k_mm])
        k_m64 = ts(B["mask64"], B["mask8"], 64.0, None, OP.mult, deps=[k_m8])
        k_rep = ts(T.rep16[:], T.mmf[:], pcol, None, OP.is_equal, deps=[k_mmf])
    zwa = ms(T.wa[:, 0:SLOTS], 0.0)
    if side_b:
        k_to = ts(T.toff[:, 0:8 * NL], T.tof[:, 0:8 * NL], pcol, None, OP.add, deps=[c_to])
        k_bd = ts(T.bd[:, 0:128 * NL], T.tl[:, 0:128 * NL], gcol, None, OP.is_equal, deps=[c_bd, k_pgf])

    for q, qn, src, out, sem in ((Y, "y", T.rini, l_in[0], "dl"), (A, "a", T.rinj, l_in[1], "dl2")):
        wait(q, qn, [("rawin", nraw), ("dself", 32) if tself else None])
        dma(q, qn, out, src[0:NL], sem)
    l_i, l_j = ("dl", 16), ("dl2", 16)
    if is_owner:
        wait(Y, "y", [l_i, l_j])
        for a in range(1, 4):
            t_ta = dma(Y, "y", T.sta[:, 2048 * a:2048 * a + 2048], T.ta[:, 2048 * a:2048 * a + 2048], "dta1")
        for a in range(4):
            t_tb = dma(Y, "y", T.stb[:, 2048 * a:2048 * a + 2048], T.tb[:, 2048 * a:2048 * a + 2048], "dtb")

    banks = [T.sc0, T.un]
    bank_free = [None, None]

    def places(l, dep):
        t1 = ts(B["x"], l, 63, None, OP.bitwise_and, deps=[dep])
        t2 = ts(B["xh"], l, 6, 127, OP.logical_shift_right, OP.bitwise_and)
        vcopy(B["lo"], B["x"], deps=[t1])
        return vcopy(B["hi"], B["xh"], deps=[t2])

    def keys(mine):
        t = ts(T.h96[:, 0:2 * NC], T.lij[:, 0:2 * NC], 13, None, OP.logical_shift_right, deps=[l_i, l_j])
        h = [T.h96[:, 0:NC], T.h96[:, NC:2 * NC]]
        t = ts(B["tk"], h[mine], float(me), 16.0, OP.not_equal, OP.mult, deps=[t])
        return tt(B["key"], B["tk"], h[1 - mine], OP.max, deps=[t])

    def unwrap(lo, hi, out, blk, dep):
        bk = banks[blk % 2]
        for k in range(4):
            r = 4 * blk + k
            o = bk[:, NC * k:NC * k + NC]
            mm(o, T.zz[:, 132 * r + 1:132 * r + 129], hi, True, False, deps=[dep, k_z, bank_free[blk % 2]])
            last = mm(o, T.zz[:, 132 * r:132 * r + 128], lo, False, True)
        for k in range(4):
            r = 4 * blk + k
            t = act(out[:, r:16 * NC:16], bk[:, NC * k:NC * k + NC], deps=[last])
        bank_free[blk % 2] = t
        return t

    def one_hots(key, dep):
        toks = []
        for c in range(NR):
            o = ts(T.oh[:, 4 + NS * c:4 + NS * c + NC], key, float(c), None, OP.is_equal, deps=[dep, k_oh])
            if c % 4 == 3:
                x = 2 + NB * (c // 4)
                out = T.cum[:, 512 * (c // 4):512 * (c // 4) + NB]
                mm(out, T.tri[:], T.oh[:, x:x + NB], True, False, deps=[o, k_tri, k_trc])
                toks.append(mm(out, T.trc[:], T.oh[:, x - 1:x - 1 + NB], False, True))
        return toks

    def dumps():
        d = tt(B["dmp"], B["tk"], B["dumpc"], OP.mult, deps=[k_du])
        mm(T.sc1[:, 0:NC], T.idf[:], B["dmp"], True, False, deps=[d, k_idf])
        mm(T.sc1[:, 0:NC], T.id5[:], B["key"], False, False, deps=[k_id5])

    def scans(toks):
        m = []
        for k in range(3):
            o = (T.ofp, T.sm, T.ofp)[k][:, 0:NB]
            wait(V, "v", [toks[k], k_mb])
            s = vt(V.tensor_tensor_scan(o, T.maskb[:, 0:NB], T.cum[:, 512 * k:512 * k + NB], 0.0, OP.mult, OP.add))
            m.append(tt(T.xq[:, NB * k:NB * k + NB], o, T.oh[:, 2 + NB * k:2 + NB * k + NB], OP.mult, deps=[s]))
        return m

    def sums(k, m):
        for c in range(4 * k, 4 * k + 4):
            p = mm(T.sc1[:, 0:NC], T.idh[:], T.xq[:, NS * c + 2:NS * c + 2 + NC], False, c == NR - 1, deps=[m, k_idh])
        return p

    def slots(p, sl):
        if up:
            return vcopy(sl[:, 0:NC], T.sc1[:, 0:NC], deps=[p])
        return ts(sl[:, 0:NC], T.sc1[:, 0:NC], float(CAP - 1), None, OP.add, deps=[p])

    def scatter(win, sl, vals, deps):
        wait(V, "v", deps)
        return vt(V.tensor_copy(win[:, 0:SLOTS + 16 * NC].indirect(sl[:, 0:NC]), vals[:, 0:16 * NC]))

    def wrap1(win, dep, classes, out):
        for i, ch in enumerate([4 * c + q for c in classes for q in range(4)]):
            t = mm(out[:, 2 * i:2 * i + 2], win[:, 128 * ch:128 * ch + 128], T.sel[:, 0:2], deps=[dep, k_sel])
        return t

    def wrap2(x, n, out, dep):
        for b in range(8):
            o = out[:, b:32 * n:8]
            mm(o, T.lb[:, 256 * b:256 * b + 128], x[:, 0:8 * n:2], True, False, deps=[dep, k_lb])
            t = mm(o, T.lb[:, 256 * b + 128:256 * b + 256], x[:, 1:8 * n:2], False, True)
        return t

    def turn(dep):
        t = ts(B["t5"], T.sc1[:, 0:NC], 0.0 if up else float(CAP - 1), None, OP.add, deps=[dep])
        wait(V, "v", [t, k_to, k_bd])
        t = vt(V.tensor_copy(T.tl[:, 0:128 * NL], B["t5"].indirect(T.toff[:, 0:8 * NL])))
        t = tt(T.tl[:, 0:128 * NL], T.tl[:, 0:128 * NL], T.bd[:, 0:128 * NL], OP.mult, deps=[t])
        for c in range(NL):
            p = mm(T.un[:, c:NC:NL], T.tl[:, 128 * c:128 * c + 128], B["mask16"], deps=[t, u])
        return vcopy(T.slt[:, 0:NC], T.un[:, 0:NC], deps=[p])

    def send(out, src, name, dep):
        rid, pid = dst(own)
        mask = sum(bits(topo.mask(core, own))[:NE])
        wait(g, "g", [dep])
        g.remote_dma(out_ap=out, in_ap=src, remote_sem=S[name], local_sem=S["xsent"], pid=pid, routing_id=rid,
                     dma_engine_mask=mask)
        return NE

    def arrival(h):
        if h == me:
            return 0.0
        i = order[h].index(me)
        if topo.chip(cores[h]) == topo.chip(own):
            return 3.0 + 0.1 * i
        return (2.0 if i < 3 else 0.0) + 1.2 * i + (2.0 if (cores[h], own) in relay else 0.0)

    row = sorted(range(NR), key=lambda h: (arrival(h), h))

    mine = 1 if side_b else 0
    k_key = keys(mine)
    toks = one_hots(B["key"], k_key)
    dumps()
    k_pl = places(l_in[mine], (l_i, l_j)[mine])
    m = scans(toks)
    for blk in range(4):
        u = unwrap(B["lo"], B["hi"], T.va, blk, k_pl)
        if blk < 3:
            p = sums(blk, m[blk])
    sl = slots(p, T.sla)
    sc = scatter(T.wa, T.sla, T.va, [sl, u, zwa])
    n = 0
    X1, X2 = (0, 8 * PA), (8 * PA, 96)
    seq = row if side_b else order[me]
    w1 = wrap1(T.wa, sc, seq[:PA], T.sm)
    w2 = wrap1(T.wa, sc, seq[PA:], T.cum)
    if not is_owner:
        nx = {"partner": "xpa", "mate": "xmb", "helper": "xpb"}[role]
        for (a, e), ps, wt, sfx in ((X1, T.sm, w1, ""), (X2, T.cum, w2, "2")):
            x = vcopy(T.xa[:, a:e], ps[:, 0:e - a], deps=[wt])
            n += send(T[nx][:, a:e], T.xa[:, a:e], nx + sfx, x)
        if side_b:
            n += send((T.slt if up else T.slp)[:, 0:NC], T.slt[:, 0:NC], "slm" if up else "slp", turn(x))
        jobs = [(s, d) for (s, d), r in relay.items() if r == core]
        for s, d in sorted(jobs, key=lambda sd: order[cores.index(sd[0])].index(cores.index(sd[1]))):
            h, k = cores.index(s), slot_at_relay(cores, topo, d)
            g.wait_ge(S["rl%d" % k], 8)
            rid, pid = dst(d)
            g.remote_dma(out_ap=T.rb[:, CAP * h:CAP * h + CAP], in_ap=T.rb[:, CAP * k:CAP * k + CAP],
                         remote_sem=S["pay%d" % h], local_sem=S["rlsent"], pid=pid, routing_id=rid,
                         dma_engine_mask=topo.mask(core, d))
        wait(g, "g", [("rlsent", 8 * len(jobs)) if jobs else None, ("xsent", n)])
        wait(g, "g", [(k, cnt[k]) for k in ("v", "a", "p", "gp")])
        return

    for b in range(8):
        for w in range(2):
            c = (80 if w else 96) + b
            k_lb = act(T.lb[:, 128 * (2 * b + w):128 * (2 * b + w) + 128], T.rep16[:], deps=[k_rep, k_m64],
                       scale=T.f16[:, c:c + 1])
    k_of = ms(T.onesf[:], 1.0)
    k_p8 = ts(B["p8"], B["ip"], 7, None, OP.bitwise_and)
    zsw = ms(T.sw[:, SLOTS:WIN], 0.0)
    k_p8f = vcopy(B["p8f"], B["p8"], deps=[k_p8])
    k_seg = tt(B["seg8"], B["p8f"], B["ir"], OP.is_equal, deps=[k_p8f])

    def offsets_a(a, e, ps, wt, name, out):
        x = tt(T.xa[:, a:e], ps[:, 0:e - a], T.xpa[:, a:e], OP.add, deps=[wt, (name, NE)])
        return wrap2(T.xa[:, a:e], (e - a) // 8, out, x)

    def offsets_a2(a, e, out, p):
        return vcopy(T.offa[:, 4 * a:4 * e], out[:, 0:4 * (e - a)], deps=[p])

    o_a = offsets_a2(*X1, T.ofp, offsets_a(*X1, T.sm, w1, "xpa", T.ofp))
    out2 = T.cum[:, 512:1024]
    full = {}
    nsentp = 0
    sent = []
    noff = 0
    for i, b in enumerate(order[me]):
        d = cores[b]
        off = topo.chip(d) != topo.chip(core)
        noff += off
        on_a = b == me or (off and noff in (1, 3, 4, 5, 7))
        src = T.sta[:, 0:RC].indirect(T.offa[:, 32 * i:32 * i + 32])
        blk = T.sb[:, CAP * b:CAP * b + CAP]
        if i == PA:
            o_a = offsets_a2(*X2, out2, p2)
        deps = [o_a, t_ta0, t_ta]
        full[b] = act(blk, src, deps=deps) if on_a else vcopy(blk, src, deps=deps)
        if i == 1:
            p2 = offsets_a(*X2, T.cum, w2, "xpa2", out2)
        if b == me:
            continue
        wait(g, "g", [full[b]])
        out, sem, to = T.rb[:, CAP * me:CAP * me + CAP], "pay%d" % me, d
        if (core, d) in relay:
            k, to = slot_at_relay(cores, topo, d), relay[core, d]
            out, sem = T.rb[:, CAP * k:CAP * k + CAP], "rl%d" % k
        mask = topo.mask(core, to)
        lsem = "psent"
        if off:
            if noff > WINDOW:
                wait(g, "g", [sent[noff - 1 - WINDOW]])
            lsem = "ps%d" % (noff - 1)
            sent.append((lsem, 8))
        else:
            mask &= ~mo
            nsentp += 8
        rid, pid = dst(to)
        g.remote_dma(out_ap=out, in_ap=blk, remote_sem=S[sem], local_sem=S[lsem], pid=pid, routing_id=rid,
                     dma_engine_mask=mask)

    def offsets_b(a, e, sfx):
        x = tt(T.xb[:, a:e], T.xpb[:, a:e], T.xmb[:, a:e], OP.add, deps=[("xpb" + sfx, NE), ("xmb" + sfx, NE)])
        return wrap2(T.xb[:, a:e], (e - a) // 8, T.ofp[:, 4 * a:4 * e], x)

    def offsets_b2(a, e, p):
        return vcopy(T.offb[:, 4 * a:4 * e], T.ofp[:, 4 * a:4 * e], deps=[p])

    o_b = offsets_b2(*X1, offsets_b(*X1, ""))
    scs = [T.sc0[:], T.sc1[:], T.un[:]] + [T.cum[:, 512 * k:512 * k + 512] for k in range(3)]
    pm_ = [None, None]
    pc_ = [u, sl, u, sl, sl, sl]
    n = 0
    for nh, h in enumerate(row):
        blk = T.sb if h == me else T.rb
        ready = full[me] if h == me else ("pay%d" % h, 8)
        for a, e in ([(0, CAP // 2), (CAP // 2, CAP)] if h == row[-1] else [(0, CAP)]):
            k, j = n % 2, n % 6
            n += 1
            pr = T.prod[:, CAP * k:CAP * k + e - a]
            wait(V, "v", [o_b, t_tb, ready, pm_[k]])
            t = vt(V.tensor_tensor(pr, T.stb[:, 0:RC].indirect(T.offb[:, 32 * nh + a // 16:32 * nh + e // 16]),
                                   blk[:, CAP * h + a:CAP * h + e], OP.mult))
            pm_[k] = mm(scs[j][:, 0:e - a], T.onesf[:], pr, deps=[t, k_of, pc_[j]])
            if nh == 0:
                p_b2 = offsets_b(*X2, "2")
            if nh == 2:
                o_b = offsets_b2(*X2, p_b2)
            pc_[j] = act(T.sw[:, CAP * h + a:CAP * h + e], scs[j][:, 0:e - a], deps=[pm_[k]])

    wait(V, "v", pc_ + [zsw, ("slm", NE)])
    f0 = vt(V.tensor_copy(T.r0[:], T.sw[:, 0:WIN].indirect(T.slt[:, 0:16 * LISTS[0]])))
    wait(A, "a", pc_ + [zsw, ("slp", NE)])
    f1 = at(A.activation(T.r1[:], T.sw[:, 0:WIN].indirect(T.slp[:, 0:16 * LISTS[1]]), AF.Copy))
    dma(Y, "y", T.dres[0:first], T.r0[0:128:16, :], "dd0", deps=[f0])
    dma(A, "a", T.dres[first:NR], T.r1[0:128:16, :], "dd1", deps=[f1])
    td = [("dd0", cnt["dd0"]), ("dd1", cnt["dd1"])]
    wait(g, "g", td)
    offr = [b for b in range(NR) if topo.chip(cores[b]) != topo.chip(core)]
    onr = [b for b in range(NR) if topo.chip(cores[b]) == topo.chip(core) and b != me]
    nres = 0
    for L, mask, w in ((offr, mo, 1), (onr, mn, 2)):
        bl = bits(mask)
        tr = []
        for n, b in enumerate(L):
            rid, pid = dst(cores[b])
            tr.append(RemoteDMATransfer(dst_ids=[DstId(rid=rid, pnc=pid)], dma_engine_mask=sum(bl[w * n:w * n + w]),
                                        remote_sem=S["resin"], srcs=[T.dres[b]], dsts=[T.resd[me]], alu_op=0))
            nres += w
        g.remote_dma_fused(tr, local_sem=S["ressent"])
    t_me = dma(Y, "y", T.resd[me], T.dres[me], "dd2", deps=td)
    t_x = dma(Y, "y", T.res[:], T.resd[:], "dx", deps=[t_me, ("resin", nres)])
    py = mm(T.ofp[0:8, 0:256], T.f16[0:96, 112:120], T.res[:], deps=[t_x, k_seg])
    ty = vcopy(T.ys[:], T.ofp[0:8, 0:256], deps=[py])
    dma(Y, "y", T.y[:], T.ys[:], "dy", deps=[ty])
    wait(g, "g", [("dy", 16), ("rawsent", 4 * EL), ("rawsent2", 2 * EL), ("psent", nsentp), ("ressent", nres), t_ta0] + sent)
    wait(g, "g", [(k, cnt[k]) for k in ("v", "a", "p", "gp")])


def slot_at_relay(cores, topo, d):
    return [c for c in cores if topo.chip(c) == topo.chip(d)].index(d)
